import numpy as np
import ml_dtypes


def mxq(x, axis, fmt="e4m3"):
    dtype, down = {"e4m3": (ml_dtypes.float8_e4m3fn, 7), "e5m2": (ml_dtypes.float8_e5m2, 14)}[fmt]
    v = np.moveaxis(np.asarray(x, np.float32).astype(ml_dtypes.bfloat16).astype(np.float64), axis, -1)
    blocks = v.reshape(v.shape[:-1] + (-1, 32))
    amax = np.abs(blocks).max(-1, keepdims=True)
    byte = np.maximum(np.where(amax > 0, np.frexp(amax)[1] - 1 + 127, 0) - down, 1)
    scale = np.exp2(byte - 127.0)
    codes = (blocks / scale).astype(np.float32).astype(dtype).astype(np.float64)
    return np.moveaxis((codes * scale).reshape(v.shape), -1, axis)


WIDE = False


def mx_kscale(k):
    if not WIDE:
        return np.ones(k)
    levels = np.array([10, -10, 5, -5, 0])
    if k % 512:
        return np.exp2(np.random.permutation(np.resize(levels, k // 32))).repeat(32)
    a = np.empty((k // 512, 16))
    for p in range(k // 512):
        a[p, :8] = np.random.permutation(np.resize(levels, 8))
        for g in range(8):
            far = levels[np.abs(levels - a[p, g]) >= 10]
            a[p, g + 8] = far[np.random.randint(len(far))]
    return np.exp2(a.ravel()).repeat(32)


BF16 = ml_dtypes.bfloat16


def bf(x):
    return np.asarray(x, np.float32).astype(BF16)


def f64(x):
    return np.asarray(x).astype(np.float64)


B, T, C, D, P = 2, 2, 512, 512, 512


def draw0():
    s = mx_kscale(C)
    t = mx_kscale(D)
    k = np.random.standard_normal((B, T, C, D)) / np.sqrt(C) * s[:, None]
    w = np.random.standard_normal((B, T, C, D)) * 2.0 / np.sqrt(D) / s[:, None]
    u = np.random.standard_normal((B, T, C, P)) / s[:, None]
    g = np.random.uniform(0.7, 1.0, (B, T, D))
    ga = (1.0 + 0.1 * np.random.standard_normal(D)) * t
    gb = (1.0 + 0.1 * np.random.standard_normal(D)) / t
    return {"k": bf(k), "w": bf(w), "u": bf(u), "g": bf(g), "ga": bf(ga), "gb": bf(gb)}


def chunk_affine_maps(k, w, u, g):
    kt = mxq(k, 2, "e4m3").transpose(0, 1, 3, 2)
    kw = kt @ mxq(w, 2, "e4m3")
    h = kt @ mxq(u, 2, "e4m3")
    m = np.eye(g.shape[-1]) * g[..., :, None] - kw
    return m, h


def core(k, w, u, g, ga, gb):
    m, h = chunk_affine_maps(f64(k), f64(w), f64(u), f64(g))
    m2 = mxq(m[:, 1] * f64(ga)[None, None, :], 2, "e4m3")
    m1 = mxq(m[:, 0] * f64(gb)[None, :, None], 1, "e4m3")
    h1 = mxq(h[:, 0] * f64(gb)[None, :, None], 1, "e4m3")
    mm = m2 @ m1
    hh = (m2 @ h1) + h[:, 1]
    return mm, hh


def e4m3fn_bytes(y):
    return np.clip(np.asarray(y, np.float64), -448.0, 448.0).astype(np.float32).astype(ml_dtypes.float8_e4m3fn).view(np.uint8)


def e4m3fn_values(b):
    return np.asarray(b, np.uint8).view(ml_dtypes.float8_e4m3fn).astype(np.float64)


def setup_inputs():
    d = draw0()
    x0 = np.asarray(d['w']).astype(np.float64)
    s = (np.max(np.abs(x0), axis=(0, 1, 3), keepdims=True) / 448.0).astype(np.float32)
    out = {}
    for k, v in d.items():
        if k == 'w':
            out['w_bytes'] = e4m3fn_bytes(x0 / s.astype(np.float64))
            out['w_scale'] = s
        else:
            out[k] = v
    return out


def reference(k, w_bytes, w_scale, u, g, ga, gb):
    return core(k, e4m3fn_values(w_bytes) * w_scale.astype(np.float64), u, g, ga, gb)

@@ -1,0 +1,261 @@
+from contextlib import ExitStack
+
+import concourse.mybir as mybir
+from concourse.masks import make_identity
+
+F32 = mybir.dt.float32
+BF16 = mybir.dt.bfloat16
+U32 = mybir.dt.uint32
+U8 = mybir.dt.uint8
+FP8 = mybir.dt.float8_e4m3fn
+FP8X4 = mybir.dt.float8_e4m3fn_x4
+COPY = mybir.ActivationFunctionType.Copy
+MULT = mybir.AluOpType.mult
+ADD = mybir.AluOpType.add
+
+P = 128
+J = 4
+N = 512
+FLOPS = 12 * 2 * 512 * 512 * 512
+
+SEQ = """
+Wd002S Wd000V Wd001V Wd003S Ki00aV Wd010S Ki00bV Wd011S Wd012V Wi00aV Wd013S Ki01aS
+Wi00bV Ut00aP Wi01aV Wi01bS Ut00bP Ki01bV Ut01aP Kq00V Ui00aS Wq01V Ut01bP Ui00bS
+Wd101V Ui01aS Uq00V Wd110S Wd111V Hm00P Wq00V Wd112S Hm01P Hm02P Ki11aV Wd113S
+Hm03P Ui01bS Hd00V Mm000P Mm001P Ki11bS Hd01V Mm002P Mm003P Hd02V Ut11aP Md000S
+Hd03V Md001S Ut11bP Wi11aV Md002S Ut10aP Hq0V Md003S Wi11bS Uq01V Ut10bP Mp000V
+Mp001V Mp002V Wd100S Mp003V Kq11V Mi00aS Mi00bV Ki10bV Wd102S Kq01V Wd103S Ui10aS
+Wq11V Mm010P Mm011P Ui10bS Wi10aV Mm012P Md010S Mm013P Wi10bV Md011S Uq10V Md012S
+Md013S Wq10V Ui11aS Mp010V Mp011V Ui11bS Mp012V Mm110P Mp013V Mq00V Ki10aS Mm111P
+Mi01aV Mm112P Mm113P Mi01bV Md110S Md111S Kq10V Md112S Mq01V Mm100P Md113S Mm101P
+Uq11V Md100S Mm102P Md101S Mm103P Mp100V Mp110V Md102S Mp111V Om00P Mp101V Mp112V
+Md103S Om01P Mp102V Mp113V Om02P Od00S Mp103V Om03P Mi11aV Hm10P Od01S Hm11P
+Mi10bV Od02S Hm12P Mi11bV Hm13P Od03S Gm00P Mi10aS Hd10V Gm01P Mq11V Gm02P
+Gd00S Hd11V Gm03P Gd01S Mq10V Gd02S Hd12V Om10P Gd03S Om11P Hd13V Om12P
+Od10S Om13P Hq1V Od11S Od13V Od12S Gm10P Gm11P Gd10S Gm12P Gd11V Gm13P
+Gd12V Gd13S
+""".split()
+
+
+def tile_gateddeltacontextparallelaffinemerge_kernel(tc, k, w_bytes, w_scale, u, g, ga, gb, out_0, out_1):
+    nc = tc.nc
+
+    with ExitStack() as ctx:
+        keep = ctx.enter_context(tc.tile_pool(name="keep", bufs=1))
+        stage = ctx.enter_context(tc.tile_pool(name="stage", bufs=4))
+        grp = ctx.enter_context(tc.tile_pool(name="grp", bufs=8))
+        psum = ctx.enter_context(tc.psum_pool(name="psum", bufs=8))
+        ctx.enter_context(tc.manual_schedule())
+
+        k_sb, w_sb, u_sb, codes, scales = {}, {}, {}, {}, {}
+        for b in range(2):
+            for c in range(2):
+                x = str(b) + str(c)
+                k_sb[x] = keep.tile([P, J, N], BF16, name="k_sb" + x, align_bytes=64)
+                w_sb[x] = keep.tile([P, J, N], U8, name="w_sb" + x, align_bytes=64)
+                u_sb[x] = keep.tile([P, J, N], BF16, name="u_sb" + x, align_bytes=64)
+        for key in ("K00", "K01", "K10", "K11", "W00", "W01", "W10", "W11", "U00", "U01", "U10", "U11", "M00", "M01", "M10", "M11", "H0", "H1"):
+            codes[key] = keep.tile([P, N], U32, name="codes" + key, align_bytes=64)
+            scales[key] = keep.tile([P, N], U8, name="scales" + key, align_bytes=64)
+        outs = {}
+        for key in ("O0", "O1", "G0", "G1"):
+            outs[key] = keep.tile([P, 4, N], F32, name="out" + key, align_bytes=64)
+
+        wscale = keep.tile([P, J], F32)
+        gain_b = keep.tile([P, J], BF16)
+        gain_a = keep.tile([P, J], BF16)
+        gates = keep.tile([P, 4, J], BF16)
+        neg_gain = keep.tile([P, 2, J], F32)
+        gb_f = keep.tile([P, J], F32)
+        gate_gain = keep.tile([P, 4, J], F32)
+        ident = keep.tile([P, P], F32)
+        ident_bf = keep.tile([P, P], BF16)
+        diag = keep.tile([P, 4, J, P], F32)
+
+        nc.scalar.dma_start(out=wscale[:], in_=w_scale[0, 0].rearrange("(p j) o -> p (j o)", j=J))
+
+        def load_k(x):
+            nc.sync.dma_start(out=k_sb[x][:], in_=k[int(x[0]), int(x[1])].rearrange("(p j) d -> p j d", j=J))
+
+        def load_w(x):
+            nc.sync.dma_start(out=w_sb[x][:], in_=w_bytes[int(x[0]), int(x[1])].rearrange("(p j) d -> p j d", j=J))
+
+        def load_u(x):
+            nc.sync.dma_start(out=u_sb[x][:], in_=u[int(x[0]), int(x[1])].rearrange("(p j) d -> p j d", j=J))
+
+        for b in ("0", "1"):
+            load_w(b + "0")
+            load_k(b + "0")
+            load_w(b + "1")
+            load_k(b + "1")
+            load_u(b + "0")
+            load_u(b + "1")
+        nc.gpsimd.dma_start(out=gain_b[:], in_=gb.rearrange("(p t) -> p t", t=J))
+        nc.gpsimd.dma_start(out=gain_a[:], in_=ga.rearrange("(p t) -> p t", t=J))
+        nc.gpsimd.dma_start(out=gates[:], in_=g.rearrange("b c (p t) -> p (b c) t", t=J))
+
+        make_identity(nc, ident_bf[:])
+        make_identity(nc, ident[:])
+        nc.gpsimd.tensor_scalar(out=neg_gain[:, 0, :], in0=gain_b[:], scalar1=-1.0, scalar2=0.0, op0=MULT, op1=ADD)
+        nc.gpsimd.tensor_scalar(out=neg_gain[:, 1, :], in0=gain_a[:], scalar1=-1.0, scalar2=0.0, op0=MULT, op1=ADD)
+        nc.gpsimd.tensor_scalar(out=gb_f[:], in0=gain_b[:], scalar1=1.0, scalar2=0.0, op0=MULT, op1=ADD)
+        for bc in range(4):
+            nc.gpsimd.tensor_tensor(out=gate_gain[:, bc, :], in0=gates[:, bc, :], in1=(gain_b, gain_a)[bc % 2][:], op=MULT)
+            for t in range(J):
+                nc.gpsimd.tensor_scalar(
+                    out=diag[:, bc, t, :], in0=ident[:], scalar1=gate_gain[:, bc, t : t + 1], scalar2=0.0, op0=MULT, op1=ADD
+                )
+
+        wide, grouped, planes, banks = {}, {}, {}, {}
+
+        def copy(e, out, in_):
+            if e == "V":
+                nc.vector.tensor_copy(out=out, in_=in_)
+            else:
+                nc.scalar.copy(out=out, in_=in_)
+
+        def get_grouped(key):
+            if key not in grouped:
+                tile = grp.tile([P, J * N], BF16, name="grouped", align_bytes=64)
+                grouped[key] = tile
+            return grouped[key]
+
+        def widen(x, j, e):
+            if x not in wide:
+                wide[x] = stage.tile([P, J, N], BF16, name="wide", align_bytes=64)
+            src = w_sb[x][:, j, :].bitcast(FP8)
+            if e == "V":
+                nc.vector.tensor_scalar(out=wide[x][:, j, :], in0=src, scalar1=wscale[:, j : j + 1], scalar2=None, op0=MULT)
+            else:
+                nc.scalar.activation(out=wide[x][:, j, :], in_=src, func=COPY, scale=wscale[:, j : j + 1])
+
+        def permuted(key, src, h, e):
+            m = slice(64 * h, 64 * h + 64)
+            dst = get_grouped(key)[:].rearrange("p (t m j) -> p m j t", t=4, j=J)[:, m]
+            copy(e, dst, src[:].rearrange("p j (m t) -> p m j t", t=4)[:, m])
+
+        def plain(key, src, h, e):
+            cols = slice(256 * h, 256 * h + 256)
+            dst = get_grouped(key)[:, 1024 * h : 1024 * h + 1024].rearrange("p (c i t) -> p c t i", i=4, t=J)
+            copy(e, dst, src[:, :, cols].rearrange("p t (c i) -> p c t i", i=4))
+
+        def quantize(key):
+            nc.vector.quantize_mx(out=codes[key][:].bitcast(FP8X4), scales=scales[key][:], in_=grouped[key][:])
+
+        def bank(key, dtype=F32):
+            width = N if dtype == F32 else 2 * N
+            tile = psum.tile([P, width], dtype, name="bank")
+            banks[key] = tile
+            return tile
+
+        def mm(out, a, ta, bkey, cols, start=True, stop=True):
+            ac = slice(P * ta, P * ta + P)
+            nc.tensor.matmul_mx(
+                out=out,
+                lhsT=codes[a][:, ac].bitcast(FP8X4),
+                lhsT_scale=scales[a][:, ac],
+                rhs=codes[bkey][:, cols].bitcast(FP8X4),
+                rhs_scale=scales[bkey][:, cols],
+                start=start,
+                stop=stop,
+            )
+
+        full = slice(0, N)
+        half = {"a": 0, "b": 1}
+        stored = {}
+        for item in SEQ:
+            kind, x, i, e = item[:2], item[2:4], item[4:-1], item[-1]
+            bcol = item[2]
+            if kind == "Wd":
+                widen(x, int(i), e)
+            elif kind == "Ki":
+                permuted("K" + x, k_sb[x], half[i], e)
+            elif kind == "Wi":
+                permuted("W" + x, wide[x], half[i], e)
+            elif kind in ("Kq", "Wq", "Uq", "Mq"):
+                quantize(kind[0] + x)
+            elif kind == "Hq":
+                quantize("H" + bcol)
+            elif kind == "Ut":
+                tile = bank(item[:-1], BF16)
+                h = half[i]
+                for q in range(2):
+                    c0 = 256 * h + 128 * q
+                    nc.tensor.matmul(
+                        out=tile[:, 512 * q : 512 * q + 512].rearrange("p (n j) -> p n j", j=J),
+                        lhsT=ident_bf[:],
+                        rhs=u_sb[x][:, :, c0 : c0 + 128].rearrange("p j n -> p n j"),
+                        start=True,
+                        stop=True,
+                    )
+            elif kind == "Ui":
+                h = half[i]
+                key = "Ut" + x + i
+                if key in banks:
+                    copy(e, get_grouped("U" + x)[:, 1024 * h : 1024 * h + 1024], banks[key][:])
+                else:
+                    plain("U" + x, u_sb[x], h, e)
+            elif kind == "Mm":
+                t = int(i)
+                a, r = ("K" + x, "W" + x) if x[1] == "0" else ("W" + x, "K" + x)
+                mm(bank(item[:-1])[:], a, t, r, full)
+            elif kind == "Md":
+                t = int(i)
+                if x not in planes:
+                    planes[x] = stage.tile([P, J, N], BF16, name="plane", align_bytes=64)
+                sc = neg_gain[:, int(x[1]), t : t + 1]
+                src = banks["Mm" + x + i]
+                if t > 0:
+                    nc.scalar.activation(out=planes[x][:, t, : P * t], in_=src[:, : P * t], func=COPY, scale=sc)
+                if t < 3:
+                    nc.scalar.activation(out=planes[x][:, t, P * t + P :], in_=src[:, P * t + P :], func=COPY, scale=sc)
+            elif kind == "Mp":
+                t = int(i)
+                cols = slice(P * t, P * t + P)
+                bc = 2 * int(x[0]) + int(x[1])
+                nc.vector.scalar_tensor_tensor(
+                    out=planes[x][:, t, cols],
+                    in0=banks["Mm" + x + i][:, cols],
+                    scalar=neg_gain[:, int(x[1]), t : t + 1],
+                    in1=diag[:, bc, t, :],
+                    op0=MULT,
+                    op1=ADD,
+                )
+            elif kind == "Mi":
+                plain("M" + x, planes[x], half[i], e)
+            elif kind == "Hm":
+                r = int(item[3])
+                tile = bank(item[:-1])
+                for t in range(4):
+                    mm(tile[:, P * t : P * t + P], "K" + bcol + "0", t, "U" + bcol + "0", slice(P * r, P * r + P))
+            elif kind == "Hd":
+                r = int(item[3])
+                nc.vector.tensor_tensor(
+                    out=get_grouped("H" + bcol)[:, 512 * r : 512 * r + 512].rearrange("p (n t) -> p n t", t=J),
+                    in0=banks["Hm" + bcol + item[3]][:].rearrange("p (t n) -> p n t", t=J),
+                    in1=gb_f[:].unsqueeze(1).to_broadcast([P, P, J]),
+                    op=MULT,
+                )
+            elif kind == "Om":
+                s = int(item[3])
+                mm(bank(item[:-1])[:], "M" + bcol + "1", s, "M" + bcol + "0", full)
+            elif kind == "Gm":
+                s = int(item[3])
+                tile = bank(item[:-1])
+                mm(tile[:], "K" + bcol + "1", s, "U" + bcol + "1", full, start=True, stop=False)
+                mm(tile[:], "M" + bcol + "1", s, "H" + bcol, full, start=False, stop=True)
+            elif kind in ("Od", "Gd"):
+                s = int(item[3])
+                key = kind[0] + bcol
+                src = banks[kind[0] + "m" + bcol + item[3]][:]
+                dst = outs[key][:, s, :]
+                if kind == "Od":
+                    src = src.rearrange("p (s m) -> p m s", s=4)
+                    dst = dst.rearrange("p (m s) -> p m s", s=4)
+                copy(e, dst, src)
+                dram = (out_0 if kind == "Od" else out_1)[int(bcol)].rearrange("(p s) n -> p s n", s=4)
+                done = stored.setdefault(key, set())
+                done.add(s)
+                pair = s // 2
+                if 2 * pair in done and 2 * pair + 1 in done:
+                    nc.sync.dma_start(out=dram[:, 2 * pair : 2 * pair + 2], in_=outs[key][:, 2 * pair : 2 * pair + 2, :])

@@ -19,21 +19,21 @@ N = 512
 FLOPS = 12 * 2 * 512 * 512 * 512
 
 SEQ = """
-Wd002S Wd000V Wd001V Wd003S Ki00aV Wd010S Ki00bV Wd011S Wd012V Wi00aV Wd013S Ki01aS
-Wi00bV Ut00aP Wi01aV Wi01bS Ut00bP Ki01bV Ut01aP Kq00V Ui00aS Wq01V Ut01bP Ui00bS
-Wd101V Ui01aS Uq00V Wd110S Wd111V Hm00P Wq00V Wd112S Hm01P Hm02P Ki11aV Wd113S
-Hm03P Ui01bS Hd00V Mm000P Mm001P Ki11bS Hd01V Mm002P Mm003P Hd02V Ut11aP Md000S
-Hd03V Md001S Ut11bP Wi11aV Md002S Ut10aP Hq0V Md003S Wi11bS Uq01V Ut10bP Mp000V
-Mp001V Mp002V Wd100S Mp003V Kq11V Mi00aS Mi00bV Ki10bV Wd102S Kq01V Wd103S Ui10aS
-Wq11V Mm010P Mm011P Ui10bS Wi10aV Mm012P Md010S Mm013P Wi10bV Md011S Uq10V Md012S
-Md013S Wq10V Ui11aS Mp010V Mp011V Ui11bS Mp012V Mm110P Mp013V Mq00V Ki10aS Mm111P
-Mi01aV Mm112P Mm113P Mi01bV Md110S Md111S Kq10V Md112S Mq01V Mm100P Md113S Mm101P
-Uq11V Md100S Mm102P Md101S Mm103P Mp100V Mp110V Md102S Mp111V Om00P Mp101V Mp112V
-Md103S Om01P Mp102V Mp113V Om02P Od00S Mp103V Om03P Mi11aV Hm10P Od01S Hm11P
-Mi10bV Od02S Hm12P Mi11bV Hm13P Od03S Gm00P Mi10aS Hd10V Gm01P Mq11V Gm02P
-Gd00S Hd11V Gm03P Gd01S Mq10V Gd02S Hd12V Om10P Gd03S Om11P Hd13V Om12P
-Od10S Om13P Hq1V Od11S Od13V Od12S Gm10P Gm11P Gd10S Gm12P Gd11V Gm13P
-Gd12V Gd13S
+Wd000S Wd001V Wd002V Wd003V Ki00bS Ki00aV Vx00 Wd012V Wi00aV Wd010S Kq00V Wd011S Ki01aV
+Wd013S Ut00aP Wi01bS Ki01bV Ut00bP Wi01aV Ui00aS Kq01V Ut01aP Wd102S Wq01V Ui00bS
+Ut01bP Ki10bV Ui01aS Uq00V Mm010P Wd110S Mm011P Wd111V Ui01bS Hm00P Ki11bV Md010S
+Hm01P Uq01V Md011S Hm02P Hm03P Wd112S Mp010V Mp011V Hd00V Mm012P Wd113S Mm013P
+Hd01V Md012S Ut11aP Wi11aV Md013S Ki11aS Ut11bP Mp012V Ui11aV Mp013V Ut10aP Wi11bV
+Ui11bS Mi01aS Kq11V Ut10bP Wq11V Mi01bS Hd02V Hd03V Mm110P Ki10aS Uq11V Mm111P
+Mm112P Mq01V Mm113P Md110S Hq0V Md111S Kq10V Gm00P Md112S Mp110V Md113S Mp111V
+Gm01P Mp112V Ui10aS Wd100V Mp113V Wd101V Gd00S Gm02P Mi11aV Gd01S Mi11bV Ui10bS
+Wi00bV Gd02S Gm03P Wd103S Uq10V Gd03S Mq11V Hm10P Wi10aS Wq00V Hm11P Hm12P
+Hd10V Mm000P Wi10bS Hd11V Mm001P Mm002P Hd12V Mm003P Md000S Wq10V Hm13P Md001S
+Mp000V Md002S Mm100P Hd13V Mm101P Md003S Mp001V Mp002V Mm102P Md100S Hq1V Mm103P
+Md101S Mp003V Gm10P Mp100V Md102S Mp101V Mi00aV Md103S Gm11P Gd10S Mi00bV Gm12P
+Gd11S Mp102V Mp103V Mq00V Gm13P Gd12S Mi10aV Om00P Gd13S Mi10bV Om01P Od00S
+Om02P Om03P Mq10V Od01S Od03V Od02S Om10P Om11P Od10S Om12P Od11V Om13P
+Od12V Od13S
 """.split()
 
 
@@ -62,9 +62,9 @@ def tile_gateddeltacontextparallelaffinemerge_kernel(tc, k, w_bytes, w_scale, u,
             outs[key] = keep.tile([P, 4, N], F32, name="out" + key, align_bytes=64)
 
         wscale = keep.tile([P, J], F32)
-        gain_b = keep.tile([P, J], BF16)
-        gain_a = keep.tile([P, J], BF16)
-        gates = keep.tile([P, 4, J], BF16)
+        vec_rows = keep.tile([P, N], BF16)
+        vec_perm = keep.tile([P, N], BF16)
+        vecs = keep.tile([P, J, 8], F32)
         neg_gain = keep.tile([P, 2, J], F32)
         gb_f = keep.tile([P, J], F32)
         gate_gain = keep.tile([P, 4, J], F32)
@@ -72,7 +72,12 @@ def tile_gateddeltacontextparallelaffinemerge_kernel(tc, k, w_bytes, w_scale, u,
         ident_bf = keep.tile([P, P], BF16)
         diag = keep.tile([P, 4, J, P], F32)
 
+        nc.vector.memset(vec_rows[:], 0.0)
         nc.scalar.dma_start(out=wscale[:], in_=w_scale[0, 0].rearrange("(p j) o -> p (j o)", j=J))
+
+        nc.scalar.dma_start(out=vec_rows[0:4, :], in_=g.rearrange("b c d -> (b c) d"))
+        nc.scalar.dma_start(out=vec_rows[4:5, :], in_=gb.rearrange("(o d) -> o d", o=1))
+        nc.scalar.dma_start(out=vec_rows[5:6, :], in_=ga.rearrange("(o d) -> o d", o=1))
 
         def load_k(x):
             nc.sync.dma_start(out=k_sb[x][:], in_=k[int(x[0]), int(x[1])].rearrange("(p j) d -> p j d", j=J))
@@ -90,21 +95,29 @@ def tile_gateddeltacontextparallelaffinemerge_kernel(tc, k, w_bytes, w_scale, u,
             load_k(b + "1")
             load_u(b + "0")
             load_u(b + "1")
-        nc.gpsimd.dma_start(out=gain_b[:], in_=gb.rearrange("(p t) -> p t", t=J))
-        nc.gpsimd.dma_start(out=gain_a[:], in_=ga.rearrange("(p t) -> p t", t=J))
-        nc.gpsimd.dma_start(out=gates[:], in_=g.rearrange("b c (p t) -> p (b c) t", t=J))
-
         make_identity(nc, ident_bf[:])
         make_identity(nc, ident[:])
-        nc.gpsimd.tensor_scalar(out=neg_gain[:, 0, :], in0=gain_b[:], scalar1=-1.0, scalar2=0.0, op0=MULT, op1=ADD)
-        nc.gpsimd.tensor_scalar(out=neg_gain[:, 1, :], in0=gain_a[:], scalar1=-1.0, scalar2=0.0, op0=MULT, op1=ADD)
-        nc.gpsimd.tensor_scalar(out=gb_f[:], in0=gain_b[:], scalar1=1.0, scalar2=0.0, op0=MULT, op1=ADD)
-        for bc in range(4):
-            nc.gpsimd.tensor_tensor(out=gate_gain[:, bc, :], in0=gates[:, bc, :], in1=(gain_b, gain_a)[bc % 2][:], op=MULT)
-            for t in range(J):
-                nc.gpsimd.tensor_scalar(
-                    out=diag[:, bc, t, :], in0=ident[:], scalar1=gate_gain[:, bc, t : t + 1], scalar2=0.0, op0=MULT, op1=ADD
-                )
+
+        def vectors():
+            nc.vector.tensor_copy(
+                out=vec_perm[:].rearrange("p (t g r) -> p t g r", t=4, r=8), in_=vec_rows[:].rearrange("p (g t r) -> p t g r", t=4, r=8)
+            )
+            vec_bank = psum.tile([P, 2 * N], BF16, name="bank")
+            for t in range(4):
+                nc.tensor.transpose(vec_bank[:, P * t : P * t + P], vec_perm[:, P * t : P * t + P], ident_bf[:])
+            nc.vector.tensor_copy(
+                out=vecs[:, :, 0:6], in_=vec_bank[:, : 4 * P].rearrange("p (t v) -> p t v", t=4)[:, :, 0:6]
+            )
+            for c in range(2):
+                nc.gpsimd.tensor_scalar(out=neg_gain[:, c, :], in0=vecs[:, :, 4 + c], scalar1=-1.0, scalar2=0.0, op0=MULT, op1=ADD)
+            nc.gpsimd.tensor_scalar(out=gb_f[:], in0=vecs[:, :, 4], scalar1=1.0, scalar2=0.0, op0=MULT, op1=ADD)
+            for bc in range(4):
+                nc.gpsimd.tensor_tensor(out=gate_gain[:, bc, :], in0=vecs[:, :, bc], in1=vecs[:, :, 4 + bc % 2], op=MULT)
+            for bc in range(4):
+                for t in range(J):
+                    nc.gpsimd.tensor_scalar(
+                        out=diag[:, bc, t, :], in0=ident[:], scalar1=gate_gain[:, bc, t : t + 1], scalar2=0.0, op0=MULT, op1=ADD
+                    )
 
         wide, grouped, planes, banks = {}, {}, {}, {}
 
@@ -130,9 +143,8 @@ def tile_gateddeltacontextparallelaffinemerge_kernel(tc, k, w_bytes, w_scale, u,
                 nc.scalar.activation(out=wide[x][:, j, :], in_=src, func=COPY, scale=wscale[:, j : j + 1])
 
         def permuted(key, src, h, e):
-            m = slice(64 * h, 64 * h + 64)
-            dst = get_grouped(key)[:].rearrange("p (t m j) -> p m j t", t=4, j=J)[:, m]
-            copy(e, dst, src[:].rearrange("p j (m t) -> p m j t", t=4)[:, m])
+            dst = get_grouped(key)[:].rearrange("p (t g r j) -> p t g r j", t=4, r=8, j=J)[:, 2 * h : 2 * h + 2]
+            copy(e, dst, src[:].rearrange("p j (g t r) -> p t g r j", t=4, r=8)[:, 2 * h : 2 * h + 2])
 
         def plain(key, src, h, e):
             cols = slice(256 * h, 256 * h + 256)
@@ -166,12 +178,14 @@ def tile_gateddeltacontextparallelaffinemerge_kernel(tc, k, w_bytes, w_scale, u,
         for item in SEQ:
             kind, x, i, e = item[:2], item[2:4], item[4:-1], item[-1]
             bcol = item[2]
-            if kind == "Wd":
+            if kind == "Vx":
+                vectors()
+            elif kind == "Wd":
                 widen(x, int(i), e)
             elif kind == "Ki":
-                permuted("K" + x, k_sb[x], half[i], e)
+                (permuted if x[1] == "0" else plain)("K" + x, k_sb[x], half[i], e)
             elif kind == "Wi":
-                permuted("W" + x, wide[x], half[i], e)
+                (permuted if x[1] == "1" else plain)("W" + x, wide[x], half[i], e)
             elif kind in ("Kq", "Wq", "Uq", "Mq"):
                 quantize(kind[0] + x)
             elif kind == "Hq":
@@ -205,19 +219,20 @@ def tile_gateddeltacontextparallelaffinemerge_kernel(tc, k, w_bytes, w_scale, u,
                     planes[x] = stage.tile([P, J, N], BF16, name="plane", align_bytes=64)
                 sc = neg_gain[:, int(x[1]), t : t + 1]
                 src = banks["Mm" + x + i]
+                src = src[:].rearrange("p (g c) -> p g c", c=32)
+                dst = planes[x][:, t, :].rearrange("p (g c) -> p g c", c=32)
                 if t > 0:
-                    nc.scalar.activation(out=planes[x][:, t, : P * t], in_=src[:, : P * t], func=COPY, scale=sc)
+                    nc.scalar.activation(out=dst[:, :, : 8 * t], in_=src[:, :, : 8 * t], func=COPY, scale=sc)
                 if t < 3:
-                    nc.scalar.activation(out=planes[x][:, t, P * t + P :], in_=src[:, P * t + P :], func=COPY, scale=sc)
+                    nc.scalar.activation(out=dst[:, :, 8 * t + 8 :], in_=src[:, :, 8 * t + 8 :], func=COPY, scale=sc)
             elif kind == "Mp":
                 t = int(i)
-                cols = slice(P * t, P * t + P)
                 bc = 2 * int(x[0]) + int(x[1])
                 nc.vector.scalar_tensor_tensor(
-                    out=planes[x][:, t, cols],
-                    in0=banks["Mm" + x + i][:, cols],
+                    out=planes[x][:, t, :].rearrange("p (g c) -> p g c", c=32)[:, :, 8 * t : 8 * t + 8],
+                    in0=banks["Mm" + x + i][:].rearrange("p (g c) -> p g c", c=32)[:, :, 8 * t : 8 * t + 8],
                     scalar=neg_gain[:, int(x[1]), t : t + 1],
-                    in1=diag[:, bc, t, :],
+                    in1=diag[:, bc, t, :].rearrange("p (g r) -> p g r", r=8),
                     op0=MULT,
                     op1=ADD,
                 )
@@ -249,11 +264,8 @@ def tile_gateddeltacontextparallelaffinemerge_kernel(tc, k, w_bytes, w_scale, u,
                 key = kind[0] + bcol
                 src = banks[kind[0] + "m" + bcol + item[3]][:]
                 dst = outs[key][:, s, :]
-                if kind == "Od":
-                    src = src.rearrange("p (s m) -> p m s", s=4)
-                    dst = dst.rearrange("p (m s) -> p m s", s=4)
                 copy(e, dst, src)
-                dram = (out_0 if kind == "Od" else out_1)[int(bcol)].rearrange("(p s) n -> p s n", s=4)
+                dram = (out_0 if kind == "Od" else out_1)[int(bcol)].rearrange("(s p) n -> p s n", p=P)
                 done = stored.setdefault(key, set())
                 done.add(s)
                 pair = s // 2

@@ -19,21 +19,21 @@ N = 512
 FLOPS = 12 * 2 * 512 * 512 * 512
 
 SEQ = """
-Wd000S Wd001V Wd002V Wd003V Ki00bS Ki00aV Vx00 Wd012V Wi00aV Wd010S Kq00V Wd011S Ki01aV
-Wd013S Ut00aP Wi01bS Ki01bV Ut00bP Wi01aV Ui00aS Kq01V Ut01aP Wd102S Wq01V Ui00bS
-Ut01bP Ki10bV Ui01aS Uq00V Mm010P Wd110S Mm011P Wd111V Ui01bS Hm00P Ki11bV Md010S
-Hm01P Uq01V Md011S Hm02P Hm03P Wd112S Mp010V Mp011V Hd00V Mm012P Wd113S Mm013P
-Hd01V Md012S Ut11aP Wi11aV Md013S Ki11aS Ut11bP Mp012V Ui11aV Mp013V Ut10aP Wi11bV
-Ui11bS Mi01aS Kq11V Ut10bP Wq11V Mi01bS Hd02V Hd03V Mm110P Ki10aS Uq11V Mm111P
-Mm112P Mq01V Mm113P Md110S Hq0V Md111S Kq10V Gm00P Md112S Mp110V Md113S Mp111V
-Gm01P Mp112V Ui10aS Wd100V Mp113V Wd101V Gd00S Gm02P Mi11aV Gd01S Mi11bV Ui10bS
-Wi00bV Gd02S Gm03P Wd103S Uq10V Gd03S Mq11V Hm10P Wi10aS Wq00V Hm11P Hm12P
-Hd10V Mm000P Wi10bS Hd11V Mm001P Mm002P Hd12V Mm003P Md000S Wq10V Hm13P Md001S
-Mp000V Md002S Mm100P Hd13V Mm101P Md003S Mp001V Mp002V Mm102P Md100S Hq1V Mm103P
-Md101S Mp003V Gm10P Mp100V Md102S Mp101V Mi00aV Md103S Gm11P Gd10S Mi00bV Gm12P
-Gd11S Mp102V Mp103V Mq00V Gm13P Gd12S Mi10aV Om00P Gd13S Mi10bV Om01P Od00S
-Om02P Om03P Mq10V Od01S Od03V Od02S Om10P Om11P Od10S Om12P Od11V Om13P
-Od12V Od13S
+Wd000S Wd001V Wd002V Wd003V Ki00aS Ki00bV Vx00 Wd010V Wd011V Wd013S Wd012V Kq00V Ki01bS
+Wi01bV Ki01aV Wi01aS Wi00aV Ui00aS Ui01aV Wq01V Ui00bS Wd100V Kq01V Wi00bV Wd101S
+Mm010P Wd102S Uq00V Mm011P Wd103S Mm012P Ki11bV Ki11aS Mm013P Wq00V Hm00P Wi10bV
+Hm01P Ui01bS Mm000P Kq11V Mm001P Hd00V Md000S Hd01V Md001S Mp000V Wi10aS Ki10aV
+Mp001V Wd110V Md010S Wd112V Uq01V Md011S Md012S Wq10V Md013S Mp010V Mp011V Ki10bS
+Mm002P Mp012V Mp013V Ui10aV Mm003P Mi01bS Mi01aV Hm02P Hm03P Kq10V Md002S G100P
+Mq01aV Mm100P Md003S Mq01bV Mm101P Mp002V Wd111S Hd02V Mm102P Mm103P Wd113S Mp003V
+Hd03V G101P Md100S G102P Wi11bV Wi11aS G103P Mp100V Hq0V Md101S Mi00bV Gm00P
+Md102S Gm01P Mp101V Md103S Gm02P Wq11V Gm03P Mi00aS Mq00bV Mp102V Mp103V Gd01V
+Gd00S Mq00aV Gd03S Gd02V Mm110P Ui11bS Ui10bV Mm111P Mm112P Ui11aV Md110S Mm113P
+Uq10V Md111S Om00P Mp110V Md112S Om01P Uq11V Hm10P Md113S Hm11P Mp111V Od00S
+Mp112V Hm12P Mp113V Hm13P Hd10V Od01S G110P Hd11V G111P Mi11aS G112P Hd12V
+G113P Om02P Hd13V Om03P Mi11bS Mq11aV Hq1V Od02S Mq11bV Gm10P Mi10aV Od03S
+Gm11P Gm12P Gd10S Mi10bV Gm13P Gd11S Mq10aV Mq10bV Gd12S Om10P Gd13S Om11P
+Om12P Od10S Om13P Od11S Od13V Od12S
 """.split()
 
 
@@ -154,6 +154,12 @@ def tile_gateddeltacontextparallelaffinemerge_kernel(tc, k, w_bytes, w_scale, u,
         def quantize(key):
             nc.vector.quantize_mx(out=codes[key][:].bitcast(FP8X4), scales=scales[key][:], in_=grouped[key][:])
 
+        def half_quantize(key, h):
+            cols = slice(256 * h, 256 * h + 256)
+            nc.vector.quantize_mx(
+                out=codes[key][:, cols].bitcast(FP8X4), scales=scales[key][:, cols], in_=grouped[key][:, 1024 * h : 1024 * h + 1024]
+            )
+
         def bank(key, dtype=F32):
             width = N if dtype == F32 else 2 * N
             tile = psum.tile([P, width], dtype, name="bank")
@@ -186,7 +192,9 @@ def tile_gateddeltacontextparallelaffinemerge_kernel(tc, k, w_bytes, w_scale, u,
                 (permuted if x[1] == "0" else plain)("K" + x, k_sb[x], half[i], e)
             elif kind == "Wi":
                 (permuted if x[1] == "1" else plain)("W" + x, wide[x], half[i], e)
-            elif kind in ("Kq", "Wq", "Uq", "Mq"):
+            elif kind == "Mq":
+                half_quantize("M" + x, half[i])
+            elif kind in ("Kq", "Wq", "Uq"):
                 quantize(kind[0] + x)
             elif kind == "Hq":
                 quantize("H" + bcol)
@@ -254,11 +262,13 @@ def tile_gateddeltacontextparallelaffinemerge_kernel(tc, k, w_bytes, w_scale, u,
             elif kind == "Om":
                 s = int(item[3])
                 mm(bank(item[:-1])[:], "M" + bcol + "1", s, "M" + bcol + "0", full)
+            elif kind == "G1":
+                s = int(item[3])
+                tile = bank("Gm" + item[2:-1])
+                mm(tile[:], "K" + bcol + "1", s, "U" + bcol + "1", full, start=True, stop=False)
             elif kind == "Gm":
                 s = int(item[3])
-                tile = bank(item[:-1])
-                mm(tile[:], "K" + bcol + "1", s, "U" + bcol + "1", full, start=True, stop=False)
-                mm(tile[:], "M" + bcol + "1", s, "H" + bcol, full, start=False, stop=True)
+                mm(banks[item[:-1]][:], "M" + bcol + "1", s, "H" + bcol, full, start=False, stop=True)
             elif kind in ("Od", "Gd"):
                 s = int(item[3])
                 key = kind[0] + bcol

@@ -19,21 +19,22 @@ N = 512
 FLOPS = 12 * 2 * 512 * 512 * 512
 
 SEQ = """
-Wd000S Wd001V Wd002V Wd003V Ki00aS Ki00bV Vx00 Wd010V Wd011V Wd013S Wd012V Kq00V Ki01bS
-Wi01bV Ki01aV Wi01aS Wi00aV Ui00aS Ui01aV Wq01V Ui00bS Wd100V Kq01V Wi00bV Wd101S
-Mm010P Wd102S Uq00V Mm011P Wd103S Mm012P Ki11bV Ki11aS Mm013P Wq00V Hm00P Wi10bV
-Hm01P Ui01bS Mm000P Kq11V Mm001P Hd00V Md000S Hd01V Md001S Mp000V Wi10aS Ki10aV
-Mp001V Wd110V Md010S Wd112V Uq01V Md011S Md012S Wq10V Md013S Mp010V Mp011V Ki10bS
-Mm002P Mp012V Mp013V Ui10aV Mm003P Mi01bS Mi01aV Hm02P Hm03P Kq10V Md002S G100P
-Mq01aV Mm100P Md003S Mq01bV Mm101P Mp002V Wd111S Hd02V Mm102P Mm103P Wd113S Mp003V
-Hd03V G101P Md100S G102P Wi11bV Wi11aS G103P Mp100V Hq0V Md101S Mi00bV Gm00P
-Md102S Gm01P Mp101V Md103S Gm02P Wq11V Gm03P Mi00aS Mq00bV Mp102V Mp103V Gd01V
-Gd00S Mq00aV Gd03S Gd02V Mm110P Ui11bS Ui10bV Mm111P Mm112P Ui11aV Md110S Mm113P
-Uq10V Md111S Om00P Mp110V Md112S Om01P Uq11V Hm10P Md113S Hm11P Mp111V Od00S
-Mp112V Hm12P Mp113V Hm13P Hd10V Od01S G110P Hd11V G111P Mi11aS G112P Hd12V
-G113P Om02P Hd13V Om03P Mi11bS Mq11aV Hq1V Od02S Mq11bV Gm10P Mi10aV Od03S
-Gm11P Gm12P Gd10S Mi10bV Gm13P Gd11S Mq10aV Mq10bV Gd12S Om10P Gd13S Om11P
-Om12P Od10S Om13P Od11S Od13V Od12S
+Wd002S Wd000V Wd001V Wd003S Ki00bV Ki00aS Vp00V Wi00aV Vt00P Wd010S Ki01V Wd011S
+Wd012S Ut00aP Wd013S Wi00bV Wd100S Kq01V Ut00bP Wi01aS Wi01bV Wq00V Ut01aP Ui00aS
+Kq00V Ut01bP Ui00bS Wq01V Ui01aS Mm000P Mm001P Uq00V Ui01bS Mm002P Vc00V Ge00V
+Dg00G Dg01G Md000S Md001S Uq01V Mm010P Md002S Mm011P Ki10V Mm012P Md010S Mm013P
+Md011S Mm003P Md012S Ki11bV Md013S Kq10V Md003S Wd101S Mp000V Mp001V Mp002V Hm00P
+Wd102S Mp003V Wd113V Hm01P Wd103S Mi00aV Hm02P Ki11aS Ge10V Dg10G Dg11G Mp010V
+Mp011V Mp012V Hm03P Mp013V Ut11aP Hd00V Wi10bS Ut11bP Mi01bV Ut10aP Hd01V Mi01aS
+Hd02V Ut10bP Hd03V G100P Ui11aS G101P Mi00bV G102P Ui10aS G103P Ui10bS Hq0V
+Wd110S Mq01V Wd111S Ui11bV Gm00P Wd112S Gm01P Mq00V Gm02P Gd00S Gm03P Uq10V
+Om00P Wi11bS Om01P Wi11aV Om02P Om03P Wi10aV Hm10P Gd01S Wq11V Gd02S Hm11P
+Wq10V Gd03S Hm12P Od03V Od00S Mm100P Kq11V Od01S Mm101P Hd10V Od02S Mm110P
+Hd11V Md100S Mm111P Md110S Mm112P Hd12V Mm113P Md111S Mm102P Mp100V Mp110V Mm103P
+Md112S Uq11V Hm13P Md113S Mp111V Md101S Mp112V Mp113V Hd13V Md102S Md103S Mp101V
+Mi11aV G110P Mi11bS Mp102V G111P Mp103V Hq1V G112P Mi10bS Mq11V G113P Mi10aV
+Gm10P Gm11P Gd10S Gm12P Mq10V Gm13P Gd11S Gd12V Om10P Om11P Gd13V Od10S
+Om12P Om13P Od11S Od12S Od13V
 """.split()
 
 
@@ -75,10 +76,6 @@ def tile_gateddeltacontextparallelaffinemerge_kernel(tc, k, w_bytes, w_scale, u,
         nc.vector.memset(vec_rows[:], 0.0)
         nc.scalar.dma_start(out=wscale[:], in_=w_scale[0, 0].rearrange("(p j) o -> p (j o)", j=J))
 
-        nc.scalar.dma_start(out=vec_rows[0:4, :], in_=g.rearrange("b c d -> (b c) d"))
-        nc.scalar.dma_start(out=vec_rows[4:5, :], in_=gb.rearrange("(o d) -> o d", o=1))
-        nc.scalar.dma_start(out=vec_rows[5:6, :], in_=ga.rearrange("(o d) -> o d", o=1))
-
         def load_k(x):
             nc.sync.dma_start(out=k_sb[x][:], in_=k[int(x[0]), int(x[1])].rearrange("(p j) d -> p j d", j=J))
 
@@ -88,36 +85,23 @@ def tile_gateddeltacontextparallelaffinemerge_kernel(tc, k, w_bytes, w_scale, u,
         def load_u(x):
             nc.sync.dma_start(out=u_sb[x][:], in_=u[int(x[0]), int(x[1])].rearrange("(p j) d -> p j d", j=J))
 
-        for b in ("0", "1"):
-            load_w(b + "0")
-            load_k(b + "0")
-            load_w(b + "1")
-            load_k(b + "1")
-            load_u(b + "0")
-            load_u(b + "1")
+        load_w("00")
+        load_k("00")
+        nc.sync.dma_start(out=vec_rows[0:4, :], in_=g.rearrange("b c d -> (b c) d"))
+        nc.sync.dma_start(out=vec_rows[4:5, :], in_=gb.rearrange("(o d) -> o d", o=1))
+        nc.sync.dma_start(out=vec_rows[5:6, :], in_=ga.rearrange("(o d) -> o d", o=1))
+        load_w("01")
+        load_k("01")
+        load_u("00")
+        load_w("10")
+        load_k("10")
+        load_u("01")
+        load_w("11")
+        load_k("11")
+        load_u("10")
+        load_u("11")
         make_identity(nc, ident_bf[:])
         make_identity(nc, ident[:])
-
-        def vectors():
-            nc.vector.tensor_copy(
-                out=vec_perm[:].rearrange("p (t g r) -> p t g r", t=4, r=8), in_=vec_rows[:].rearrange("p (g t r) -> p t g r", t=4, r=8)
-            )
-            vec_bank = psum.tile([P, 2 * N], BF16, name="bank")
-            for t in range(4):
-                nc.tensor.transpose(vec_bank[:, P * t : P * t + P], vec_perm[:, P * t : P * t + P], ident_bf[:])
-            nc.vector.tensor_copy(
-                out=vecs[:, :, 0:6], in_=vec_bank[:, : 4 * P].rearrange("p (t v) -> p t v", t=4)[:, :, 0:6]
-            )
-            for c in range(2):
-                nc.gpsimd.tensor_scalar(out=neg_gain[:, c, :], in0=vecs[:, :, 4 + c], scalar1=-1.0, scalar2=0.0, op0=MULT, op1=ADD)
-            nc.gpsimd.tensor_scalar(out=gb_f[:], in0=vecs[:, :, 4], scalar1=1.0, scalar2=0.0, op0=MULT, op1=ADD)
-            for bc in range(4):
-                nc.gpsimd.tensor_tensor(out=gate_gain[:, bc, :], in0=vecs[:, :, bc], in1=vecs[:, :, 4 + bc % 2], op=MULT)
-            for bc in range(4):
-                for t in range(J):
-                    nc.gpsimd.tensor_scalar(
-                        out=diag[:, bc, t, :], in0=ident[:], scalar1=gate_gain[:, bc, t : t + 1], scalar2=0.0, op0=MULT, op1=ADD
-                    )
 
         wide, grouped, planes, banks = {}, {}, {}, {}
 
@@ -143,12 +127,13 @@ def tile_gateddeltacontextparallelaffinemerge_kernel(tc, k, w_bytes, w_scale, u,
                 nc.scalar.activation(out=wide[x][:, j, :], in_=src, func=COPY, scale=wscale[:, j : j + 1])
 
         def permuted(key, src, h, e):
-            dst = get_grouped(key)[:].rearrange("p (t g r j) -> p t g r j", t=4, r=8, j=J)[:, 2 * h : 2 * h + 2]
-            copy(e, dst, src[:].rearrange("p j (g t r) -> p t g r j", t=4, r=8)[:, 2 * h : 2 * h + 2])
+            ts = slice(0, 4) if h is None else slice(2 * h, 2 * h + 2)
+            dst = get_grouped(key)[:].rearrange("p (t g r j) -> p t g r j", t=4, r=8, j=J)[:, ts]
+            copy(e, dst, src[:].rearrange("p j (g t r) -> p t g r j", t=4, r=8)[:, ts])
 
         def plain(key, src, h, e):
-            cols = slice(256 * h, 256 * h + 256)
-            dst = get_grouped(key)[:, 1024 * h : 1024 * h + 1024].rearrange("p (c i t) -> p c t i", i=4, t=J)
+            cols = slice(0, N) if h is None else slice(256 * h, 256 * h + 256)
+            dst = get_grouped(key)[:, 4 * cols.start : 4 * cols.stop].rearrange("p (c i t) -> p c t i", i=4, t=J)
             copy(e, dst, src[:, :, cols].rearrange("p t (c i) -> p c t i", i=4))
 
         def quantize(key):
@@ -179,22 +164,50 @@ def tile_gateddeltacontextparallelaffinemerge_kernel(tc, k, w_bytes, w_scale, u,
             )
 
         full = slice(0, N)
-        half = {"a": 0, "b": 1}
-        stored = {}
+        half = {"a": 0, "b": 1, "": None}
         for item in SEQ:
             kind, x, i, e = item[:2], item[2:4], item[4:-1], item[-1]
             bcol = item[2]
-            if kind == "Vx":
-                vectors()
+            if kind == "Vp":
+                nc.vector.tensor_copy(
+                    out=vec_perm[:].rearrange("p (t g r) -> p t g r", t=4, r=8),
+                    in_=vec_rows[:].rearrange("p (g t r) -> p t g r", t=4, r=8),
+                )
+            elif kind == "Vt":
+                tile = bank("Vt", BF16)
+                for t in range(4):
+                    nc.tensor.transpose(tile[:, P * t : P * t + P], vec_perm[:, P * t : P * t + P], ident_bf[:])
+            elif kind == "Vc":
+                nc.vector.tensor_copy(
+                    out=vecs[:, :, 0:6], in_=banks["Vt"][:, : 4 * P].rearrange("p (t v) -> p t v", t=4)[:, :, 0:6]
+                )
+                nc.vector.tensor_scalar(
+                    out=neg_gain[:], in0=vecs[:, :, 4:6].rearrange("p t c -> p c t"), scalar1=-1.0, scalar2=None, op0=MULT
+                )
+                nc.vector.tensor_copy(out=gb_f[:], in_=vecs[:, :, 4])
+            elif kind == "Ge":
+                b = int(x[0])
+                nc.vector.tensor_tensor(
+                    out=gate_gain[:, 2 * b : 2 * b + 2, :],
+                    in0=vecs[:, :, 2 * b : 2 * b + 2].rearrange("p t c -> p c t"),
+                    in1=vecs[:, :, 4:6].rearrange("p t c -> p c t"),
+                    op=MULT,
+                )
+            elif kind == "Dg":
+                bc = 2 * int(x[0]) + int(x[1])
+                for t in range(J):
+                    nc.gpsimd.tensor_scalar(
+                        out=diag[:, bc, t, :], in0=ident[:], scalar1=gate_gain[:, bc, t : t + 1], scalar2=0.0, op0=MULT, op1=ADD
+                    )
             elif kind == "Wd":
                 widen(x, int(i), e)
             elif kind == "Ki":
                 (permuted if x[1] == "0" else plain)("K" + x, k_sb[x], half[i], e)
             elif kind == "Wi":
                 (permuted if x[1] == "1" else plain)("W" + x, wide[x], half[i], e)
-            elif kind == "Mq":
+            elif kind == "Mq" and i:
                 half_quantize("M" + x, half[i])
-            elif kind in ("Kq", "Wq", "Uq"):
+            elif kind in ("Kq", "Wq", "Uq", "Mq"):
                 quantize(kind[0] + x)
             elif kind == "Hq":
                 quantize("H" + bcol)
@@ -204,16 +217,16 @@ def tile_gateddeltacontextparallelaffinemerge_kernel(tc, k, w_bytes, w_scale, u,
                 for q in range(2):
                     c0 = 256 * h + 128 * q
                     nc.tensor.matmul(
-                        out=tile[:, 512 * q : 512 * q + 512].rearrange("p (n j) -> p n j", j=J),
+                        out=tile[:, 512 * q : 512 * q + 512].rearrange("p (n i j) -> p n j i", j=J, i=8),
                         lhsT=ident_bf[:],
-                        rhs=u_sb[x][:, :, c0 : c0 + 128].rearrange("p j n -> p n j"),
+                        rhs=u_sb[x][:, :, c0 : c0 + 128].rearrange("p j (n i) -> p n j i", i=8),
                         start=True,
                         stop=True,
                     )
             elif kind == "Ui":
                 h = half[i]
                 key = "Ut" + x + i
-                if key in banks:
+                if i and key in banks:
                     copy(e, get_grouped("U" + x)[:, 1024 * h : 1024 * h + 1024], banks[key][:])
                 else:
                     plain("U" + x, u_sb[x], h, e)
@@ -276,8 +289,4 @@ def tile_gateddeltacontextparallelaffinemerge_kernel(tc, k, w_bytes, w_scale, u,
                 dst = outs[key][:, s, :]
                 copy(e, dst, src)
                 dram = (out_0 if kind == "Od" else out_1)[int(bcol)].rearrange("(s p) n -> p s n", p=P)
-                done = stored.setdefault(key, set())
-                done.add(s)
-                pair = s // 2
-                if 2 * pair in done and 2 * pair + 1 in done:
-                    nc.sync.dma_start(out=dram[:, 2 * pair : 2 * pair + 2], in_=outs[key][:, 2 * pair : 2 * pair + 2, :])
+                nc.sync.dma_start(out=dram[:, s, :], in_=outs[key][:, s, :])

@@ -14,279 +14,377 @@ MULT = mybir.AluOpType.mult
 ADD = mybir.AluOpType.add
 
 P = 128
-J = 4
 N = 512
-FLOPS = 12 * 2 * 512 * 512 * 512
+PACK = 4
+RUN = 8
+BATCHES = (0, 1)
+CHUNKS = ((0, 0), (0, 1), (1, 0), (1, 1))
+VEC_GB, VEC_GA = 4, 5
 
-SEQ = """
-Wd002S Wd000V Wd001V Wd003S Ki00bV Ki00aS Vp00V Wi00aV Vt00P Wd010S Ki01V Wd011S
-Wd012S Ut00aP Wd013S Wi00bV Wd100S Kq01V Ut00bP Wi01aS Wi01bV Wq00V Ut01aP Ui00aS
-Kq00V Ut01bP Ui00bS Wq01V Ui01aS Mm000P Mm001P Uq00V Ui01bS Mm002P Vc00V Ge00V
-Dg00G Dg01G Md000S Md001S Uq01V Mm010P Md002S Mm011P Ki10V Mm012P Md010S Mm013P
-Md011S Mm003P Md012S Ki11bV Md013S Kq10V Md003S Wd101S Mp000V Mp001V Mp002V Hm00P
-Wd102S Mp003V Wd113V Hm01P Wd103S Mi00aV Hm02P Ki11aS Ge10V Dg10G Dg11G Mp010V
-Mp011V Mp012V Hm03P Mp013V Ut11aP Hd00V Wi10bS Ut11bP Mi01bV Ut10aP Hd01V Mi01aS
-Hd02V Ut10bP Hd03V G100P Ui11aS G101P Mi00bV G102P Ui10aS G103P Ui10bS Hq0V
-Wd110S Mq01V Wd111S Ui11bV Gm00P Wd112S Gm01P Mq00V Gm02P Gd00S Gm03P Uq10V
-Om00P Wi11bS Om01P Wi11aV Om02P Om03P Wi10aV Hm10P Gd01S Wq11V Gd02S Hm11P
-Wq10V Gd03S Hm12P Od03V Od00S Mm100P Kq11V Od01S Mm101P Hd10V Od02S Mm110P
-Hd11V Md100S Mm111P Md110S Mm112P Hd12V Mm113P Md111S Mm102P Mp100V Mp110V Mm103P
-Md112S Uq11V Hm13P Md113S Mp111V Md101S Mp112V Mp113V Hd13V Md102S Md103S Mp101V
-Mi11aV G110P Mi11bS Mp102V G111P Mp103V Hq1V G112P Mi10bS Mq11V G113P Mi10aV
-Gm10P Gm11P Gd10S Gm12P Mq10V Gm13P Gd11S Gd12V Om10P Om11P Gd13V Od10S
-Om12P Om13P Od11S Od12S Od13V
-""".split()
+VECTOR = "vector"
+SCALAR = "scalar"
+
+FLOPS = 2 * 6 * 2 * N * N * N
 
 
-def tile_gateddeltacontextparallelaffinemerge_kernel(tc, k, w_bytes, w_scale, u, g, ga, gb, out_0, out_1):
+def tile_gateddeltacontextparallelaffinemerge_kernel(
+    tc, k, w_bytes, w_scale, u, g, ga, gb, out_0, out_1
+):
     nc = tc.nc
 
     with ExitStack() as ctx:
         keep = ctx.enter_context(tc.tile_pool(name="keep", bufs=1))
-        stage = ctx.enter_context(tc.tile_pool(name="stage", bufs=4))
-        grp = ctx.enter_context(tc.tile_pool(name="grp", bufs=8))
+        interleaved = ctx.enter_context(tc.tile_pool(name="interleaved", bufs=8))
         psum = ctx.enter_context(tc.psum_pool(name="psum", bufs=8))
         ctx.enter_context(tc.manual_schedule())
 
-        k_sb, w_sb, u_sb, codes, scales = {}, {}, {}, {}, {}
-        for b in range(2):
-            for c in range(2):
-                x = str(b) + str(c)
-                k_sb[x] = keep.tile([P, J, N], BF16, name="k_sb" + x, align_bytes=64)
-                w_sb[x] = keep.tile([P, J, N], U8, name="w_sb" + x, align_bytes=64)
-                u_sb[x] = keep.tile([P, J, N], BF16, name="u_sb" + x, align_bytes=64)
-        for key in ("K00", "K01", "K10", "K11", "W00", "W01", "W10", "W11", "U00", "U01", "U10", "U11", "M00", "M01", "M10", "M11", "H0", "H1"):
-            codes[key] = keep.tile([P, N], U32, name="codes" + key, align_bytes=64)
-            scales[key] = keep.tile([P, N], U8, name="scales" + key, align_bytes=64)
-        outs = {}
-        for key in ("O0", "O1", "G0", "G1"):
-            outs[key] = keep.tile([P, 4, N], F32, name="out" + key, align_bytes=64)
+        k_rows, u_rows, w_codes, w_wide, m_planes = {}, {}, {}, {}, {}
+        for x in CHUNKS:
+            name = "%d%d" % x
+            k_rows[x] = keep.tile([P, PACK, N], BF16, name="k_rows" + name, align_bytes=64)
+            u_rows[x] = keep.tile([P, PACK, N], BF16, name="u_rows" + name, align_bytes=64)
+            w_codes[x] = keep.tile([P, PACK, N], U8, name="w_codes" + name, align_bytes=64)
+            w_wide[x] = keep.tile([P, PACK, N], BF16, name="w_wide" + name, align_bytes=64)
+            m_planes[x] = keep.tile([P, PACK, N], BF16, name="m_planes" + name, align_bytes=64)
 
-        wscale = keep.tile([P, J], F32)
+        operands = [(kind, x) for kind in ("k", "w", "u", "m") for x in CHUNKS] + [("h", b) for b in BATCHES]
+        codes, scales = {}, {}
+        for number, key in enumerate(operands):
+            codes[key] = keep.tile([P, N], U32, name="codes%d" % number, align_bytes=64)
+            scales[key] = keep.tile([P, N], U8, name="scales%d" % number, align_bytes=64)
+
+        mm_rows, hh_rows = {}, {}
+        for b in BATCHES:
+            mm_rows[b] = keep.tile([P, 4, N], F32, name="mm_rows%d" % b, align_bytes=64)
+            hh_rows[b] = keep.tile([P, 4, N], F32, name="hh_rows%d" % b, align_bytes=64)
+
+        w_scales = keep.tile([P, PACK], F32)
         vec_rows = keep.tile([P, N], BF16)
-        vec_perm = keep.tile([P, N], BF16)
-        vecs = keep.tile([P, J, 8], F32)
-        neg_gain = keep.tile([P, 2, J], F32)
-        gb_f = keep.tile([P, J], F32)
-        gate_gain = keep.tile([P, 4, J], F32)
-        ident = keep.tile([P, P], F32)
-        ident_bf = keep.tile([P, P], BF16)
-        diag = keep.tile([P, 4, J, P], F32)
+        vec_sorted = keep.tile([P, N], BF16)
+        vecs = keep.tile([P, PACK, 8], F32)
+        neg_gain = keep.tile([P, 2, PACK], F32)
+        h_gain = keep.tile([P, PACK], F32)
+        gate_gain = keep.tile([P, 4, PACK], F32)
+        diagonal = keep.tile([P, 4, PACK, P], F32)
+        ident_f32 = keep.tile([P, P], F32)
+        ident_bf16 = keep.tile([P, P], BF16)
 
-        nc.vector.memset(vec_rows[:], 0.0)
-        nc.scalar.dma_start(out=wscale[:], in_=w_scale[0, 0].rearrange("(p j) o -> p (j o)", j=J))
+        def load(tile, dram):
+            nc.sync.dma_start(out=tile[:], in_=dram.rearrange("(p j) d -> p j d", j=PACK))
 
         def load_k(x):
-            nc.sync.dma_start(out=k_sb[x][:], in_=k[int(x[0]), int(x[1])].rearrange("(p j) d -> p j d", j=J))
-
-        def load_w(x):
-            nc.sync.dma_start(out=w_sb[x][:], in_=w_bytes[int(x[0]), int(x[1])].rearrange("(p j) d -> p j d", j=J))
+            load(k_rows[x], k[x[0], x[1]])
 
         def load_u(x):
-            nc.sync.dma_start(out=u_sb[x][:], in_=u[int(x[0]), int(x[1])].rearrange("(p j) d -> p j d", j=J))
+            load(u_rows[x], u[x[0], x[1]])
 
-        load_w("00")
-        load_k("00")
-        nc.sync.dma_start(out=vec_rows[0:4, :], in_=g.rearrange("b c d -> (b c) d"))
-        nc.sync.dma_start(out=vec_rows[4:5, :], in_=gb.rearrange("(o d) -> o d", o=1))
-        nc.sync.dma_start(out=vec_rows[5:6, :], in_=ga.rearrange("(o d) -> o d", o=1))
-        load_w("01")
-        load_k("01")
-        load_u("00")
-        load_w("10")
-        load_k("10")
-        load_u("01")
-        load_w("11")
-        load_k("11")
-        load_u("10")
-        load_u("11")
-        make_identity(nc, ident_bf[:])
-        make_identity(nc, ident[:])
+        def load_w(x):
+            load(w_codes[x], w_bytes[x[0], x[1]])
 
-        wide, grouped, planes, banks = {}, {}, {}, {}
-
-        def copy(e, out, in_):
-            if e == "V":
+        def copy(engine, out, in_):
+            if engine == VECTOR:
                 nc.vector.tensor_copy(out=out, in_=in_)
             else:
                 nc.scalar.copy(out=out, in_=in_)
 
-        def get_grouped(key):
-            if key not in grouped:
-                tile = grp.tile([P, J * N], BF16, name="grouped", align_bytes=64)
-                grouped[key] = tile
-            return grouped[key]
+        def widen(x, slots, engine):
+            for j in slots:
+                out, in_, scale = w_wide[x][:, j, :], w_codes[x][:, j, :].bitcast(FP8), w_scales[:, j : j + 1]
+                if engine == VECTOR:
+                    nc.vector.tensor_scalar(out=out, in0=in_, scalar1=scale, scalar2=None, op0=MULT)
+                else:
+                    nc.scalar.activation(out=out, in_=in_, func=COPY, scale=scale)
 
-        def widen(x, j, e):
-            if x not in wide:
-                wide[x] = stage.tile([P, J, N], BF16, name="wide", align_bytes=64)
-            src = w_sb[x][:, j, :].bitcast(FP8)
-            if e == "V":
-                nc.vector.tensor_scalar(out=wide[x][:, j, :], in0=src, scalar1=wscale[:, j : j + 1], scalar2=None, op0=MULT)
-            else:
-                nc.scalar.activation(out=wide[x][:, j, :], in_=src, func=COPY, scale=wscale[:, j : j + 1])
+        bf16_tiles = {}
 
-        def permuted(key, src, h, e):
-            ts = slice(0, 4) if h is None else slice(2 * h, 2 * h + 2)
-            dst = get_grouped(key)[:].rearrange("p (t g r j) -> p t g r j", t=4, r=8, j=J)[:, ts]
-            copy(e, dst, src[:].rearrange("p j (g t r) -> p t g r j", t=4, r=8)[:, ts])
+        def operand(key):
+            if key not in bf16_tiles:
+                tile = interleaved.tile([P, PACK * N], BF16, name="interleaved", align_bytes=64)
+                bf16_tiles[key] = tile
+            return bf16_tiles[key]
 
-        def plain(key, src, h, e):
-            cols = slice(0, N) if h is None else slice(256 * h, 256 * h + 256)
-            dst = get_grouped(key)[:, 4 * cols.start : 4 * cols.stop].rearrange("p (c i t) -> p c t i", i=4, t=J)
-            copy(e, dst, src[:, :, cols].rearrange("p t (c i) -> p c t i", i=4))
+        def interleave(key, src, engine, first=0, columns=N):
+            cols = slice(first, first + columns)
+            dst = operand(key)[:, PACK * first : PACK * (first + columns)].rearrange("p (n i v) -> p n v i", i=4, v=PACK)
+            copy(engine, dst, src[:, :, cols].rearrange("p v (n i) -> p n v i", i=4))
+
+        def interleave_sorted(key, src, engine, first=0, products=4):
+            ts = slice(first, first + products)
+            dst = operand(key)[:].rearrange("p (t q r j) -> p t q r j", t=4, r=RUN, j=PACK)[:, ts]
+            copy(engine, dst, src[:].rearrange("p j (q t r) -> p t q r j", t=4, r=RUN)[:, ts])
+
+        moved = {}
+
+        def interleave_on_tensor(key, src, first):
+            tile = psum.tile([P, 2 * N], BF16, name="bank")
+            for half in range(2):
+                cols = slice(first + P * half, first + P * half + P)
+                nc.tensor.matmul(
+                    out=tile[:, N * half : N * half + N].rearrange("p (n i j) -> p n j i", j=PACK, i=8),
+                    lhsT=ident_bf16[:],
+                    rhs=src[:, :, cols].rearrange("p j (n i) -> p n j i", i=8),
+                    start=True,
+                    stop=True,
+                )
+            moved[key, first] = tile
+
+        def collect(key, first, engine):
+            dst = operand(key)[:, PACK * first : PACK * first + 2 * N]
+            copy(engine, dst.bitcast(F32), moved[key, first][:].bitcast(F32))
 
         def quantize(key):
-            nc.vector.quantize_mx(out=codes[key][:].bitcast(FP8X4), scales=scales[key][:], in_=grouped[key][:])
+            nc.vector.quantize_mx(out=codes[key][:].bitcast(FP8X4), scales=scales[key][:], in_=operand(key)[:])
 
-        def half_quantize(key, h):
-            cols = slice(256 * h, 256 * h + 256)
-            nc.vector.quantize_mx(
-                out=codes[key][:, cols].bitcast(FP8X4), scales=scales[key][:, cols], in_=grouped[key][:, 1024 * h : 1024 * h + 1024]
-            )
-
-        def bank(key, dtype=F32):
-            width = N if dtype == F32 else 2 * N
-            tile = psum.tile([P, width], dtype, name="bank")
-            banks[key] = tile
-            return tile
-
-        def mm(out, a, ta, bkey, cols, start=True, stop=True):
-            ac = slice(P * ta, P * ta + P)
+        def product(out, stationary, tile_number, moving, cols, start=True, stop=True):
+            m_cols = slice(P * tile_number, P * tile_number + P)
             nc.tensor.matmul_mx(
                 out=out,
-                lhsT=codes[a][:, ac].bitcast(FP8X4),
-                lhsT_scale=scales[a][:, ac],
-                rhs=codes[bkey][:, cols].bitcast(FP8X4),
-                rhs_scale=scales[bkey][:, cols],
+                lhsT=codes[stationary][:, m_cols].bitcast(FP8X4),
+                lhsT_scale=scales[stationary][:, m_cols],
+                rhs=codes[moving][:, cols].bitcast(FP8X4),
+                rhs_scale=scales[moving][:, cols],
                 start=start,
                 stop=stop,
             )
 
-        full = slice(0, N)
-        half = {"a": 0, "b": 1, "": None}
-        for item in SEQ:
-            kind, x, i, e = item[:2], item[2:4], item[4:-1], item[-1]
-            bcol = item[2]
-            if kind == "Vp":
-                nc.vector.tensor_copy(
-                    out=vec_perm[:].rearrange("p (t g r) -> p t g r", t=4, r=8),
-                    in_=vec_rows[:].rearrange("p (g t r) -> p t g r", t=4, r=8),
-                )
-            elif kind == "Vt":
-                tile = bank("Vt", BF16)
-                for t in range(4):
-                    nc.tensor.transpose(tile[:, P * t : P * t + P], vec_perm[:, P * t : P * t + P], ident_bf[:])
-            elif kind == "Vc":
-                nc.vector.tensor_copy(
-                    out=vecs[:, :, 0:6], in_=banks["Vt"][:, : 4 * P].rearrange("p (t v) -> p t v", t=4)[:, :, 0:6]
-                )
-                nc.vector.tensor_scalar(
-                    out=neg_gain[:], in0=vecs[:, :, 4:6].rearrange("p t c -> p c t"), scalar1=-1.0, scalar2=None, op0=MULT
-                )
-                nc.vector.tensor_copy(out=gb_f[:], in_=vecs[:, :, 4])
-            elif kind == "Ge":
-                b = int(x[0])
-                nc.vector.tensor_tensor(
-                    out=gate_gain[:, 2 * b : 2 * b + 2, :],
-                    in0=vecs[:, :, 2 * b : 2 * b + 2].rearrange("p t c -> p c t"),
-                    in1=vecs[:, :, 4:6].rearrange("p t c -> p c t"),
-                    op=MULT,
-                )
-            elif kind == "Dg":
-                bc = 2 * int(x[0]) + int(x[1])
-                for t in range(J):
-                    nc.gpsimd.tensor_scalar(
-                        out=diag[:, bc, t, :], in0=ident[:], scalar1=gate_gain[:, bc, t : t + 1], scalar2=0.0, op0=MULT, op1=ADD
-                    )
-            elif kind == "Wd":
-                widen(x, int(i), e)
-            elif kind == "Ki":
-                (permuted if x[1] == "0" else plain)("K" + x, k_sb[x], half[i], e)
-            elif kind == "Wi":
-                (permuted if x[1] == "1" else plain)("W" + x, wide[x], half[i], e)
-            elif kind == "Mq" and i:
-                half_quantize("M" + x, half[i])
-            elif kind in ("Kq", "Wq", "Uq", "Mq"):
-                quantize(kind[0] + x)
-            elif kind == "Hq":
-                quantize("H" + bcol)
-            elif kind == "Ut":
-                tile = bank(item[:-1], BF16)
-                h = half[i]
-                for q in range(2):
-                    c0 = 256 * h + 128 * q
-                    nc.tensor.matmul(
-                        out=tile[:, 512 * q : 512 * q + 512].rearrange("p (n i j) -> p n j i", j=J, i=8),
-                        lhsT=ident_bf[:],
-                        rhs=u_sb[x][:, :, c0 : c0 + 128].rearrange("p j (n i) -> p n j i", i=8),
-                        start=True,
-                        stop=True,
-                    )
-            elif kind == "Ui":
-                h = half[i]
-                key = "Ut" + x + i
-                if i and key in banks:
-                    copy(e, get_grouped("U" + x)[:, 1024 * h : 1024 * h + 1024], banks[key][:])
+        every = slice(0, N)
+        kw_bank, h_bank, mm_bank, hh_bank = {}, {}, {}, {}
+
+        def kw_product(x):
+            for t in range(4):
+                tile = psum.tile([P, N], F32, name="bank")
+                if x[1] == 0:
+                    product(tile[:], ("k", x), t, ("w", x), every)
                 else:
-                    plain("U" + x, u_sb[x], h, e)
-            elif kind == "Mm":
-                t = int(i)
-                a, r = ("K" + x, "W" + x) if x[1] == "0" else ("W" + x, "K" + x)
-                mm(bank(item[:-1])[:], a, t, r, full)
-            elif kind == "Md":
-                t = int(i)
-                if x not in planes:
-                    planes[x] = stage.tile([P, J, N], BF16, name="plane", align_bytes=64)
-                sc = neg_gain[:, int(x[1]), t : t + 1]
-                src = banks["Mm" + x + i]
-                src = src[:].rearrange("p (g c) -> p g c", c=32)
-                dst = planes[x][:, t, :].rearrange("p (g c) -> p g c", c=32)
+                    product(tile[:], ("w", x), t, ("k", x), every)
+                kw_bank[x, t] = tile
+
+        def by_block(ap):
+            return ap.rearrange("p (q n) -> p q n", n=32)
+
+        def m_off_diagonal(x):
+            for t in range(4):
+                src, dst, scale = by_block(kw_bank[x, t][:]), by_block(m_planes[x][:, t, :]), neg_gain[:, x[1], t : t + 1]
                 if t > 0:
-                    nc.scalar.activation(out=dst[:, :, : 8 * t], in_=src[:, :, : 8 * t], func=COPY, scale=sc)
+                    nc.scalar.activation(out=dst[:, :, : RUN * t], in_=src[:, :, : RUN * t], func=COPY, scale=scale)
                 if t < 3:
-                    nc.scalar.activation(out=dst[:, :, 8 * t + 8 :], in_=src[:, :, 8 * t + 8 :], func=COPY, scale=sc)
-            elif kind == "Mp":
-                t = int(i)
-                bc = 2 * int(x[0]) + int(x[1])
+                    rest = slice(RUN * (t + 1), 32)
+                    nc.scalar.activation(out=dst[:, :, rest], in_=src[:, :, rest], func=COPY, scale=scale)
+
+        def m_diagonal(x, ts):
+            for t in ts:
+                cols = slice(RUN * t, RUN * (t + 1))
                 nc.vector.scalar_tensor_tensor(
-                    out=planes[x][:, t, :].rearrange("p (g c) -> p g c", c=32)[:, :, 8 * t : 8 * t + 8],
-                    in0=banks["Mm" + x + i][:].rearrange("p (g c) -> p g c", c=32)[:, :, 8 * t : 8 * t + 8],
-                    scalar=neg_gain[:, int(x[1]), t : t + 1],
-                    in1=diag[:, bc, t, :].rearrange("p (g r) -> p g r", r=8),
+                    out=by_block(m_planes[x][:, t, :])[:, :, cols],
+                    in0=by_block(kw_bank[x, t][:])[:, :, cols],
+                    scalar=neg_gain[:, x[1], t : t + 1],
+                    in1=diagonal[:, 2 * x[0] + x[1], t, :].rearrange("p (q r) -> p q r", r=RUN),
                     op0=MULT,
                     op1=ADD,
                 )
-            elif kind == "Mi":
-                plain("M" + x, planes[x], half[i], e)
-            elif kind == "Hm":
-                r = int(item[3])
-                tile = bank(item[:-1])
+
+        def h_product(b):
+            for part in range(4):
+                tile = psum.tile([P, N], F32, name="bank")
                 for t in range(4):
-                    mm(tile[:, P * t : P * t + P], "K" + bcol + "0", t, "U" + bcol + "0", slice(P * r, P * r + P))
-            elif kind == "Hd":
-                r = int(item[3])
+                    cols = slice(P * part, P * part + P)
+                    product(tile[:, P * t : P * t + P], ("k", (b, 0)), t, ("u", (b, 0)), cols)
+                h_bank[b, part] = tile
+
+        def h_rows(b):
+            for part in range(4):
                 nc.vector.tensor_tensor(
-                    out=get_grouped("H" + bcol)[:, 512 * r : 512 * r + 512].rearrange("p (n t) -> p n t", t=J),
-                    in0=banks["Hm" + bcol + item[3]][:].rearrange("p (t n) -> p n t", t=J),
-                    in1=gb_f[:].unsqueeze(1).to_broadcast([P, P, J]),
+                    out=operand(("h", b))[:, N * part : N * part + N].rearrange("p (n t) -> p n t", t=PACK),
+                    in0=h_bank[b, part][:].rearrange("p (t n) -> p n t", t=PACK),
+                    in1=h_gain[:].unsqueeze(1).to_broadcast([P, P, PACK]),
                     op=MULT,
                 )
-            elif kind == "Om":
-                s = int(item[3])
-                mm(bank(item[:-1])[:], "M" + bcol + "1", s, "M" + bcol + "0", full)
-            elif kind == "G1":
-                s = int(item[3])
-                tile = bank("Gm" + item[2:-1])
-                mm(tile[:], "K" + bcol + "1", s, "U" + bcol + "1", full, start=True, stop=False)
-            elif kind == "Gm":
-                s = int(item[3])
-                mm(banks[item[:-1]][:], "M" + bcol + "1", s, "H" + bcol, full, start=False, stop=True)
-            elif kind in ("Od", "Gd"):
-                s = int(item[3])
-                key = kind[0] + bcol
-                src = banks[kind[0] + "m" + bcol + item[3]][:]
-                dst = outs[key][:, s, :]
-                copy(e, dst, src)
-                dram = (out_0 if kind == "Od" else out_1)[int(bcol)].rearrange("(s p) n -> p s n", p=P)
-                nc.sync.dma_start(out=dram[:, s, :], in_=outs[key][:, s, :])
+
+        def mm_product(b):
+            for s in range(4):
+                tile = psum.tile([P, N], F32, name="bank")
+                product(tile[:], ("m", (b, 1)), s, ("m", (b, 0)), every)
+                mm_bank[b, s] = tile
+
+        def hh_open(b):
+            for s in range(4):
+                tile = psum.tile([P, N], F32, name="bank")
+                product(tile[:], ("k", (b, 1)), s, ("u", (b, 1)), every, stop=False)
+                hh_bank[b, s] = tile
+
+        def hh_close(b):
+            for s in range(4):
+                product(hh_bank[b, s][:], ("m", (b, 1)), s, ("h", b), every, start=False)
+
+        def store(bank, rows, dram, s, engine):
+            copy(engine, rows[:, s, :], bank[:])
+            nc.sync.dma_start(out=dram[P * s : P * s + P, :], in_=rows[:, s, :])
+
+        def store_mm(b, tiles, engine):
+            for s in tiles:
+                store(mm_bank[b, s], mm_rows[b], out_0[b], s, engine)
+
+        def store_hh(b, tiles, engine):
+            for s in tiles:
+                store(hh_bank[b, s], hh_rows[b], out_1[b], s, engine)
+
+        def gate_times_gain(b):
+            nc.vector.tensor_tensor(
+                out=gate_gain[:, 2 * b : 2 * b + 2, :],
+                in0=vecs[:, :, 2 * b : 2 * b + 2].rearrange("p t c -> p c t"),
+                in1=vecs[:, :, VEC_GB : VEC_GA + 1].rearrange("p t c -> p c t"),
+                op=MULT,
+            )
+
+        def diagonal_tiles(b):
+            for i in (2 * b, 2 * b + 1):
+                for t in range(4):
+                    nc.gpsimd.tensor_scalar(
+                        out=diagonal[:, i, t, :],
+                        in0=ident_f32[:],
+                        scalar1=gate_gain[:, i, t : t + 1],
+                        scalar2=0.0,
+                        op0=MULT,
+                        op1=ADD,
+                    )
+
+        a0, a1, b0, b1 = CHUNKS
+        nc.vector.memset(vec_rows[:], 0.0)
+        nc.scalar.dma_start(out=w_scales[:], in_=w_scale[0, 0].rearrange("(p j) o -> p (j o)", j=PACK))
+        load_w(a0)
+        load_k(a0)
+        nc.sync.dma_start(out=vec_rows[0:4, :], in_=g.rearrange("b c d -> (b c) d"))
+        nc.sync.dma_start(out=vec_rows[VEC_GB : VEC_GB + 1, :], in_=gb.rearrange("(o d) -> o d", o=1))
+        nc.sync.dma_start(out=vec_rows[VEC_GA : VEC_GA + 1, :], in_=ga.rearrange("(o d) -> o d", o=1))
+        load_w(a1)
+        load_k(a1)
+        load_u(a0)
+        load_w(b0)
+        load_k(b0)
+        load_u(a1)
+        load_w(b1)
+        load_k(b1)
+        load_u(b0)
+        load_u(b1)
+        make_identity(nc, ident_bf16[:])
+        make_identity(nc, ident_f32[:])
+
+
+        widen(a0, (0,), SCALAR)
+        widen(a0, (1, 2, 3), VECTOR)
+        interleave_sorted(("k", a0), k_rows[a0], SCALAR, first=0, products=2)
+        nc.vector.tensor_copy(
+            out=vec_sorted[:].rearrange("p (t q r) -> p t q r", t=4, r=RUN),
+            in_=vec_rows[:].rearrange("p (q t r) -> p t q r", t=4, r=RUN),
+        )
+        interleave(("w", a0), w_wide[a0], VECTOR)
+        vec_bank = psum.tile([P, 2 * N], BF16, name="bank")
+        for t in range(4):
+            nc.tensor.transpose(vec_bank[:, P * t : P * t + P], vec_sorted[:, P * t : P * t + P], ident_bf16[:])
+        widen(a1, (0, 1, 2, 3), SCALAR)
+        interleave(("k", a1), k_rows[a1], VECTOR)
+        interleave_on_tensor(("u", a0), u_rows[a0], 0)
+        interleave_on_tensor(("u", a0), u_rows[a0], 256)
+        nc.vector.tensor_copy(
+            out=vecs[:, :, 0 : VEC_GA + 1],
+            in_=vec_bank[:, : 4 * P].rearrange("p (t i) -> p t i", t=4)[:, :, 0 : VEC_GA + 1],
+        )
+        nc.vector.tensor_scalar(
+            out=neg_gain[:],
+            in0=vecs[:, :, VEC_GB : VEC_GA + 1].rearrange("p t c -> p c t"),
+            scalar1=-1.0,
+            scalar2=None,
+            op0=MULT,
+        )
+        nc.vector.tensor_copy(out=h_gain[:], in_=vecs[:, :, VEC_GB])
+        interleave_sorted(("k", a0), k_rows[a0], SCALAR, first=2, products=2)
+        quantize(("w", a0))
+        interleave_sorted(("w", a1), w_wide[a1], VECTOR, first=0, products=2)
+        collect(("u", a0), 0, SCALAR)
+        collect(("u", a0), 256, SCALAR)
+        quantize(("k", a0))
+        interleave_on_tensor(("u", a1), u_rows[a1], 0)
+        interleave_on_tensor(("u", a1), u_rows[a1], 256)
+        interleave_sorted(("w", a1), w_wide[a1], VECTOR, first=2, products=2)
+        widen(b0, (0,), SCALAR)
+        collect(("u", a1), 0, SCALAR)
+        quantize(("u", a0))
+
+        kw_product(a0)
+        interleave(("k", b1), k_rows[b1], SCALAR, first=256, columns=256)
+        quantize(("w", a1))
+        h_product(0)
+        widen(b1, (2, 3), VECTOR)
+        quantize(("k", a1))
+        collect(("u", a1), 256, SCALAR)
+        gate_times_gain(0)
+        diagonal_tiles(0)
+        h_rows(0)
+        m_off_diagonal(a0)
+        widen(b0, (1, 2, 3), SCALAR)
+        quantize(("u", a1))
+        gate_times_gain(1)
+        diagonal_tiles(1)
+        m_diagonal(a0, range(4))
+        kw_product(a1)
+        interleave(("w", b0), w_wide[b0], SCALAR, first=0, columns=256)
+        interleave_sorted(("k", b0), k_rows[b0], VECTOR)
+        m_off_diagonal(a1)
+        interleave(("w", b0), w_wide[b0], VECTOR, first=256, columns=256)
+        interleave_on_tensor(("u", b1), u_rows[b1], 0)
+        interleave_on_tensor(("u", b1), u_rows[b1], 256)
+        interleave_on_tensor(("k", b1), k_rows[b1], 0)
+        quantize(("k", b0))
+        quantize(("w", b0))
+        widen(b1, (0, 1), SCALAR)
+        m_diagonal(a1, range(4))
+        interleave_on_tensor(("u", b0), u_rows[b0], 0)
+        interleave_on_tensor(("u", b0), u_rows[b0], 256)
+        interleave(("m", a1), m_planes[a1], VECTOR, first=256, columns=256)
+        interleave(("m", a1), m_planes[a1], SCALAR, first=0, columns=256)
+
+        hh_open(0)
+        quantize(("h", 0))
+        interleave(("m", a0), m_planes[a0], VECTOR)
+        collect(("k", b1), 0, SCALAR)
+        collect(("u", b1), 0, SCALAR)
+        collect(("u", b1), 256, SCALAR)
+        interleave_sorted(("w", b1), w_wide[b1], VECTOR, first=0, products=2)
+        collect(("u", b0), 0, SCALAR)
+        collect(("u", b0), 256, SCALAR)
+        quantize(("m", a1))
+        quantize(("u", b1))
+        hh_close(0)
+        interleave_sorted(("w", b1), w_wide[b1], SCALAR, first=2, products=2)
+        quantize(("m", a0))
+        quantize(("u", b0))
+        store_hh(0, range(4), SCALAR)
+
+        quantize(("k", b1))
+        h_product(1)
+        quantize(("w", b1))
+        h_rows(1)
+        kw_product(b1)
+        m_off_diagonal(b1)
+        kw_product(b0)
+        m_diagonal(b1, range(4))
+        m_off_diagonal(b0)
+        mm_product(0)
+        quantize(("h", 1))
+        m_diagonal(b0, (0, 1))
+        interleave(("m", b1), m_planes[b1], VECTOR)
+
+        hh_open(1)
+        store_mm(0, range(3), SCALAR)
+        m_diagonal(b0, (2, 3))
+        quantize(("m", b1))
+        interleave(("m", b0), m_planes[b0], SCALAR, first=0, columns=256)
+        interleave(("m", b0), m_planes[b0], VECTOR, first=256, columns=256)
+        hh_close(1)
+        store_mm(0, (3,), VECTOR)
+        store_hh(1, range(3), SCALAR)
+        quantize(("m", b0))
+        store_hh(1, (3,), VECTOR)
+        mm_product(1)
+        for s in range(4):
+            store_mm(1, (s,), (SCALAR, VECTOR)[s % 2])

from contextlib import ExitStack

import concourse.mybir as mybir
from concourse.masks import make_identity

F32 = mybir.dt.float32
BF16 = mybir.dt.bfloat16
U32 = mybir.dt.uint32
U8 = mybir.dt.uint8
FP8 = mybir.dt.float8_e4m3fn
FP8X4 = mybir.dt.float8_e4m3fn_x4
COPY = mybir.ActivationFunctionType.Copy
MULT = mybir.AluOpType.mult
ADD = mybir.AluOpType.add

P = 128
N = 512
PACK = 4
RUN = 8
BATCHES = (0, 1)
CHUNKS = ((0, 0), (0, 1), (1, 0), (1, 1))
VEC_GB, VEC_GA = 4, 5

VECTOR = "vector"
SCALAR = "scalar"

FLOPS = 2 * 6 * 2 * N * N * N


def tile_gateddeltacontextparallelaffinemerge_kernel(
    tc, k, w_bytes, w_scale, u, g, ga, gb, out_0, out_1
):
    nc = tc.nc

    with ExitStack() as ctx:
        keep = ctx.enter_context(tc.tile_pool(name="keep", bufs=1))
        interleaved = ctx.enter_context(tc.tile_pool(name="interleaved", bufs=8))
        psum = ctx.enter_context(tc.psum_pool(name="psum", bufs=8))
        ctx.enter_context(tc.manual_schedule())

        k_rows, u_rows, w_codes, w_wide, m_planes = {}, {}, {}, {}, {}
        for x in CHUNKS:
            name = "%d%d" % x
            k_rows[x] = keep.tile([P, PACK, N], BF16, name="k_rows" + name, align_bytes=64)
            u_rows[x] = keep.tile([P, PACK, N], BF16, name="u_rows" + name, align_bytes=64)
            w_codes[x] = keep.tile([P, PACK, N], U8, name="w_codes" + name, align_bytes=64)
            w_wide[x] = keep.tile([P, PACK, N], BF16, name="w_wide" + name, align_bytes=64)
            m_planes[x] = keep.tile([P, PACK, N], BF16, name="m_planes" + name, align_bytes=64)

        operands = [(kind, x) for kind in ("k", "w", "u", "m") for x in CHUNKS] + [("h", b) for b in BATCHES]
        codes, scales = {}, {}
        for number, key in enumerate(operands):
            codes[key] = keep.tile([P, N], U32, name="codes%d" % number, align_bytes=64)
            scales[key] = keep.tile([P, N], U8, name="scales%d" % number, align_bytes=64)

        mm_rows, hh_rows = {}, {}
        for b in BATCHES:
            mm_rows[b] = keep.tile([P, 4, N], F32, name="mm_rows%d" % b, align_bytes=64)
            hh_rows[b] = keep.tile([P, 4, N], F32, name="hh_rows%d" % b, align_bytes=64)

        w_scales = keep.tile([P, PACK], F32)
        vec_rows = keep.tile([P, N], BF16)
        vec_sorted = keep.tile([P, N], BF16)
        vecs = keep.tile([P, PACK, 8], F32)
        neg_gain = keep.tile([P, 2, PACK], F32)
        h_gain = keep.tile([P, PACK], F32)
        gate_gain = keep.tile([P, 4, PACK], F32)
        diagonal = keep.tile([P, 4, PACK, P], F32)
        ident_f32 = keep.tile([P, P], F32)
        ident_bf16 = keep.tile([P, P], BF16)

        def load(tile, dram):
            nc.sync.dma_start(out=tile[:], in_=dram.rearrange("(p j) d -> p j d", j=PACK))

        def load_k(x):
            load(k_rows[x], k[x[0], x[1]])

        def load_u(x):
            load(u_rows[x], u[x[0], x[1]])

        def load_w(x):
            load(w_codes[x], w_bytes[x[0], x[1]])

        def copy(engine, out, in_):
            if engine == VECTOR:
                nc.vector.tensor_copy(out=out, in_=in_)
            else:
                nc.scalar.copy(out=out, in_=in_)

        def widen(x, slots, engine):
            for j in slots:
                out, in_, scale = w_wide[x][:, j, :], w_codes[x][:, j, :].bitcast(FP8), w_scales[:, j : j + 1]
                if engine == VECTOR:
                    nc.vector.tensor_scalar(out=out, in0=in_, scalar1=scale, scalar2=None, op0=MULT)
                else:
                    nc.scalar.activation(out=out, in_=in_, func=COPY, scale=scale)

        bf16_tiles = {}

        def operand(key):
            if key not in bf16_tiles:
                tile = interleaved.tile([P, PACK * N], BF16, name="interleaved", align_bytes=64)
                bf16_tiles[key] = tile
            return bf16_tiles[key]

        def interleave(key, src, engine, first=0, columns=N):
            cols = slice(first, first + columns)
            dst = operand(key)[:, PACK * first : PACK * (first + columns)].rearrange("p (n i v) -> p n v i", i=4, v=PACK)
            copy(engine, dst, src[:, :, cols].rearrange("p v (n i) -> p n v i", i=4))

        def interleave_sorted(key, src, engine, first=0, products=4):
            ts = slice(first, first + products)
            dst = operand(key)[:].rearrange("p (t q r j) -> p t q r j", t=4, r=RUN, j=PACK)[:, ts]
            copy(engine, dst, src[:].rearrange("p j (q t r) -> p t q r j", t=4, r=RUN)[:, ts])

        moved = {}

        def interleave_on_tensor(key, src, first):
            tile = psum.tile([P, 2 * N], BF16, name="bank")
            for half in range(2):
                cols = slice(first + P * half, first + P * half + P)
                nc.tensor.matmul(
                    out=tile[:, N * half : N * half + N].rearrange("p (n i j) -> p n j i", j=PACK, i=8),
                    lhsT=ident_bf16[:],
                    rhs=src[:, :, cols].rearrange("p j (n i) -> p n j i", i=8),
                    start=True,
                    stop=True,
                )
            moved[key, first] = tile

        def collect(key, first, engine):
            dst = operand(key)[:, PACK * first : PACK * first + 2 * N]
            copy(engine, dst.bitcast(F32), moved[key, first][:].bitcast(F32))

        def quantize(key):
            nc.vector.quantize_mx(out=codes[key][:].bitcast(FP8X4), scales=scales[key][:], in_=operand(key)[:])

        def product(out, stationary, tile_number, moving, cols, start=True, stop=True):
            m_cols = slice(P * tile_number, P * tile_number + P)
            nc.tensor.matmul_mx(
                out=out,
                lhsT=codes[stationary][:, m_cols].bitcast(FP8X4),
                lhsT_scale=scales[stationary][:, m_cols],
                rhs=codes[moving][:, cols].bitcast(FP8X4),
                rhs_scale=scales[moving][:, cols],
                start=start,
                stop=stop,
            )

        every = slice(0, N)
        kw_bank, h_bank, mm_bank, hh_bank = {}, {}, {}, {}

        def kw_product(x):
            for t in range(4):
                tile = psum.tile([P, N], F32, name="bank")
                if x[1] == 0:
                    product(tile[:], ("k", x), t, ("w", x), every)
                else:
                    product(tile[:], ("w", x), t, ("k", x), every)
                kw_bank[x, t] = tile

        def by_block(ap):
            return ap.rearrange("p (q n) -> p q n", n=32)

        def m_off_diagonal(x):
            for t in range(4):
                src, dst, scale = by_block(kw_bank[x, t][:]), by_block(m_planes[x][:, t, :]), neg_gain[:, x[1], t : t + 1]
                if t > 0:
                    nc.scalar.activation(out=dst[:, :, : RUN * t], in_=src[:, :, : RUN * t], func=COPY, scale=scale)
                if t < 3:
                    rest = slice(RUN * (t + 1), 32)
                    nc.scalar.activation(out=dst[:, :, rest], in_=src[:, :, rest], func=COPY, scale=scale)

        def m_diagonal(x, ts):
            for t in ts:
                cols = slice(RUN * t, RUN * (t + 1))
                nc.vector.scalar_tensor_tensor(
                    out=by_block(m_planes[x][:, t, :])[:, :, cols],
                    in0=by_block(kw_bank[x, t][:])[:, :, cols],
                    scalar=neg_gain[:, x[1], t : t + 1],
                    in1=diagonal[:, 2 * x[0] + x[1], t, :].rearrange("p (q r) -> p q r", r=RUN),
                    op0=MULT,
                    op1=ADD,
                )

        def h_product(b):
            for part in range(4):
                tile = psum.tile([P, N], F32, name="bank")
                for t in range(4):
                    cols = slice(P * part, P * part + P)
                    product(tile[:, P * t : P * t + P], ("k", (b, 0)), t, ("u", (b, 0)), cols)
                h_bank[b, part] = tile

        def h_rows(b):
            for part in range(4):
                nc.vector.tensor_tensor(
                    out=operand(("h", b))[:, N * part : N * part + N].rearrange("p (n t) -> p n t", t=PACK),
                    in0=h_bank[b, part][:].rearrange("p (t n) -> p n t", t=PACK),
                    in1=h_gain[:].unsqueeze(1).to_broadcast([P, P, PACK]),
                    op=MULT,
                )

        def mm_product(b):
            for s in range(4):
                tile = psum.tile([P, N], F32, name="bank")
                product(tile[:], ("m", (b, 1)), s, ("m", (b, 0)), every)
                mm_bank[b, s] = tile

        def hh_open(b):
            for s in range(4):
                tile = psum.tile([P, N], F32, name="bank")
                product(tile[:], ("k", (b, 1)), s, ("u", (b, 1)), every, stop=False)
                hh_bank[b, s] = tile

        def hh_close(b):
            for s in range(4):
                product(hh_bank[b, s][:], ("m", (b, 1)), s, ("h", b), every, start=False)

        def store(bank, rows, dram, s, engine):
            copy(engine, rows[:, s, :], bank[:])
            nc.sync.dma_start(out=dram[P * s : P * s + P, :], in_=rows[:, s, :])

        def store_mm(b, tiles, engine):
            for s in tiles:
                store(mm_bank[b, s], mm_rows[b], out_0[b], s, engine)

        def store_hh(b, tiles, engine):
            for s in tiles:
                store(hh_bank[b, s], hh_rows[b], out_1[b], s, engine)

        def gate_times_gain(b):
            nc.vector.tensor_tensor(
                out=gate_gain[:, 2 * b : 2 * b + 2, :],
                in0=vecs[:, :, 2 * b : 2 * b + 2].rearrange("p t c -> p c t"),
                in1=vecs[:, :, VEC_GB : VEC_GA + 1].rearrange("p t c -> p c t"),
                op=MULT,
            )

        def diagonal_tiles(b):
            for i in (2 * b, 2 * b + 1):
                for t in range(4):
                    nc.gpsimd.tensor_scalar(
                        out=diagonal[:, i, t, :],
                        in0=ident_f32[:],
                        scalar1=gate_gain[:, i, t : t + 1],
                        scalar2=0.0,
                        op0=MULT,
                        op1=ADD,
                    )

        a0, a1, b0, b1 = CHUNKS
        nc.vector.memset(vec_rows[:], 0.0)
        nc.scalar.dma_start(out=w_scales[:], in_=w_scale[0, 0].rearrange("(p j) o -> p (j o)", j=PACK))
        load_w(a0)
        load_k(a0)
        nc.sync.dma_start(out=vec_rows[0:4, :], in_=g.rearrange("b c d -> (b c) d"))
        nc.sync.dma_start(out=vec_rows[VEC_GB : VEC_GB + 1, :], in_=gb.rearrange("(o d) -> o d", o=1))
        nc.sync.dma_start(out=vec_rows[VEC_GA : VEC_GA + 1, :], in_=ga.rearrange("(o d) -> o d", o=1))
        load_w(a1)
        load_k(a1)
        load_u(a0)
        load_w(b0)
        load_k(b0)
        load_u(a1)
        load_w(b1)
        load_k(b1)
        load_u(b0)
        load_u(b1)
        make_identity(nc, ident_bf16[:])
        make_identity(nc, ident_f32[:])


        widen(a0, (0,), SCALAR)
        widen(a0, (1, 2, 3), VECTOR)
        interleave_sorted(("k", a0), k_rows[a0], SCALAR, first=0, products=2)
        nc.vector.tensor_copy(
            out=vec_sorted[:].rearrange("p (t q r) -> p t q r", t=4, r=RUN),
            in_=vec_rows[:].rearrange("p (q t r) -> p t q r", t=4, r=RUN),
        )
        interleave(("w", a0), w_wide[a0], VECTOR)
        vec_bank = psum.tile([P, 2 * N], BF16, name="bank")
        for t in range(4):
            nc.tensor.transpose(vec_bank[:, P * t : P * t + P], vec_sorted[:, P * t : P * t + P], ident_bf16[:])
        widen(a1, (0, 1, 2, 3), SCALAR)
        interleave(("k", a1), k_rows[a1], VECTOR)
        interleave_on_tensor(("u", a0), u_rows[a0], 0)
        interleave_on_tensor(("u", a0), u_rows[a0], 256)
        nc.vector.tensor_copy(
            out=vecs[:, :, 0 : VEC_GA + 1],
            in_=vec_bank[:, : 4 * P].rearrange("p (t i) -> p t i", t=4)[:, :, 0 : VEC_GA + 1],
        )
        nc.vector.tensor_scalar(
            out=neg_gain[:],
            in0=vecs[:, :, VEC_GB : VEC_GA + 1].rearrange("p t c -> p c t"),
            scalar1=-1.0,
            scalar2=None,
            op0=MULT,
        )
        nc.vector.tensor_copy(out=h_gain[:], in_=vecs[:, :, VEC_GB])
        interleave_sorted(("k", a0), k_rows[a0], SCALAR, first=2, products=2)
        quantize(("w", a0))
        interleave_sorted(("w", a1), w_wide[a1], VECTOR, first=0, products=2)
        collect(("u", a0), 0, SCALAR)
        collect(("u", a0), 256, SCALAR)
        quantize(("k", a0))
        interleave_on_tensor(("u", a1), u_rows[a1], 0)
        interleave_on_tensor(("u", a1), u_rows[a1], 256)
        interleave_sorted(("w", a1), w_wide[a1], VECTOR, first=2, products=2)
        widen(b0, (0,), SCALAR)
        collect(("u", a1), 0, SCALAR)
        quantize(("u", a0))

        kw_product(a0)
        interleave(("k", b1), k_rows[b1], SCALAR, first=256, columns=256)
        quantize(("w", a1))
        h_product(0)
        widen(b1, (2, 3), VECTOR)
        quantize(("k", a1))
        collect(("u", a1), 256, SCALAR)
        gate_times_gain(0)
        diagonal_tiles(0)
        h_rows(0)
        m_off_diagonal(a0)
        widen(b0, (1, 2, 3), SCALAR)
        quantize(("u", a1))
        gate_times_gain(1)
        diagonal_tiles(1)
        m_diagonal(a0, range(4))
        kw_product(a1)
        interleave(("w", b0), w_wide[b0], SCALAR, first=0, columns=256)
        interleave_sorted(("k", b0), k_rows[b0], VECTOR)
        m_off_diagonal(a1)
        interleave(("w", b0), w_wide[b0], VECTOR, first=256, columns=256)
        interleave_on_tensor(("u", b1), u_rows[b1], 0)
        interleave_on_tensor(("u", b1), u_rows[b1], 256)
        interleave_on_tensor(("k", b1), k_rows[b1], 0)
        quantize(("k", b0))
        quantize(("w", b0))
        widen(b1, (0, 1), SCALAR)
        m_diagonal(a1, range(4))
        interleave_on_tensor(("u", b0), u_rows[b0], 0)
        interleave_on_tensor(("u", b0), u_rows[b0], 256)
        interleave(("m", a1), m_planes[a1], VECTOR, first=256, columns=256)
        interleave(("m", a1), m_planes[a1], SCALAR, first=0, columns=256)

        hh_open(0)
        quantize(("h", 0))
        interleave(("m", a0), m_planes[a0], VECTOR)
        collect(("k", b1), 0, SCALAR)
        collect(("u", b1), 0, SCALAR)
        collect(("u", b1), 256, SCALAR)
        interleave_sorted(("w", b1), w_wide[b1], VECTOR, first=0, products=2)
        collect(("u", b0), 0, SCALAR)
        collect(("u", b0), 256, SCALAR)
        quantize(("m", a1))
        quantize(("u", b1))
        hh_close(0)
        interleave_sorted(("w", b1), w_wide[b1], SCALAR, first=2, products=2)
        quantize(("m", a0))
        quantize(("u", b0))
        store_hh(0, range(4), SCALAR)

        quantize(("k", b1))
        h_product(1)
        quantize(("w", b1))
        h_rows(1)
        kw_product(b1)
        m_off_diagonal(b1)
        kw_product(b0)
        m_diagonal(b1, range(4))
        m_off_diagonal(b0)
        mm_product(0)
        quantize(("h", 1))
        m_diagonal(b0, (0, 1))
        interleave(("m", b1), m_planes[b1], VECTOR)

        hh_open(1)
        store_mm(0, range(3), SCALAR)
        m_diagonal(b0, (2, 3))
        quantize(("m", b1))
        interleave(("m", b0), m_planes[b0], SCALAR, first=0, columns=256)
        interleave(("m", b0), m_planes[b0], VECTOR, first=256, columns=256)
        hh_close(1)
        store_mm(0, (3,), VECTOR)
        store_hh(1, range(3), SCALAR)
        quantize(("m", b0))
        store_hh(1, (3,), VECTOR)
        mm_product(1)
        for s in range(4):
            store_mm(1, (s,), (SCALAR, VECTOR)[s % 2])
